import numpy as np
import ml_dtypes


def mxq(x, axis, fmt="e4m3"):
    dtype, down = {"e4m3": (ml_dtypes.float8_e4m3fn, 7), "e5m2": (ml_dtypes.float8_e5m2, 14)}[fmt]
    v = np.moveaxis(np.asarray(x, np.float32).astype(ml_dtypes.bfloat16).astype(np.float64), axis, -1)
    blocks = v.reshape(v.shape[:-1] + (-1, 32))
    amax = np.abs(blocks).max(-1, keepdims=True)
    byte = np.maximum(np.where(amax > 0, np.frexp(amax)[1] - 1 + 127, 0) - down, 1)
    scale = np.exp2(byte - 127.0)
    codes = (blocks / scale).astype(np.float32).astype(dtype).astype(np.float64)
    return np.moveaxis((codes * scale).reshape(v.shape), -1, axis)


WIDE = False


def mx_kscale(k):
    if not WIDE:
        return np.ones(k)
    levels = np.array([10, -10, 5, -5, 0])
    if k % 512:
        return np.exp2(np.random.permutation(np.resize(levels, k // 32))).repeat(32)
    a = np.empty((k // 512, 16))
    for p in range(k // 512):
        a[p, :8] = np.random.permutation(np.resize(levels, 8))
        for g in range(8):
            far = levels[np.abs(levels - a[p, g]) >= 10]
            a[p, g + 8] = far[np.random.randint(len(far))]
    return np.exp2(a.ravel()).repeat(32)


def f64(x):
    return np.asarray(x).astype(np.float64)


def striped(idx):
    return np.tile(idx.reshape(-1, 16).T, (8, 1)).astype(np.uint16)


def unstriped(offs):
    return offs[:16].T.reshape(-1).astype(np.int64)


E2M1 = np.array([0.0, 0.5, 1.0, 1.5, 2.0, 3.0, 4.0, 6.0, -0.0, -0.5, -1.0, -1.5, -2.0, -3.0, -4.0, -6.0])


def pack_weight(w, fmt):
    k, n = w.shape
    w = f64(np.asarray(w, np.float32).astype(ml_dtypes.bfloat16)).reshape(k // 32, 32, n)
    amax = np.abs(w).max(1)
    if fmt == "e4m3":
        byte = np.frexp(amax)[1] - 1 + 127 - 7
    else:
        mant, ex = np.frexp(amax / 6.0)
        byte = np.where(mant > 0.5, ex, ex - 1) + 127
    byte = np.clip(np.where(amax > 0, byte, 1), 1, 254)
    scaled = (w * np.exp2(127.0 - byte)[:, None, :]).reshape(k, n).astype(np.float32)
    by_word = np.ascontiguousarray(scaled.reshape(k // 512, 128, 4, n).transpose(0, 1, 3, 2))
    if fmt == "e4m3":
        words = by_word.astype(ml_dtypes.float8_e4m3fn).view(np.uint8)
    else:
        c = by_word.astype(ml_dtypes.float4_e2m1fn).view(np.uint8) & 0xF
        words = (c[..., 0::2] | (c[..., 1::2] << 4)).reshape(k // 512, 128, 2 * n)
    return np.ascontiguousarray(words), np.ascontiguousarray(byte.astype(np.uint8).reshape(k // 512, 16, n))


def unpack_weight(words, scales, fmt):
    g, _, n = scales.shape
    words = np.ascontiguousarray(words).reshape(g, 128, n, -1)
    if fmt == "e4m3":
        vals = words.view(ml_dtypes.float8_e4m3fn).astype(np.float64)
    else:
        nib = np.empty((g, 128, n, 4), np.uint8)
        nib[..., 0::2] = words & 0xF
        nib[..., 1::2] = words >> 4
        vals = E2M1[nib]
    vals = vals * np.repeat(np.exp2(scales.astype(np.float64) - 127.0), 8, axis=1)[..., None]
    return vals.transpose(0, 1, 3, 2).reshape(g * 512, n)


def gelu(v):
    return 0.5 * v * (1.0 + np.tanh(np.sqrt(2.0 / np.pi) * (v + 0.044715 * v**3)))


K, T, E, C, H, N = 1024, 512, 12, 128, 512, 128
TOP = 3


def by_expert(wq, xq):
    return np.concatenate([wq[e].T @ xq[:, e * C:(e + 1) * C] for e in range(E)], axis=1)


def setup_inputs():
    n = np.random.standard_normal
    s = mx_kscale(K)[:, None]
    u = mx_kscale(H)
    deal = np.repeat(np.arange(E), C).reshape(TOP, T)[:, np.random.permutation(T)]
    deal = np.take_along_axis(deal, np.argsort(np.random.rand(TOP, T), axis=0), axis=0)
    for _ in range(8):
        s_, t_ = np.random.permutation(T).reshape(2, -1); r = np.random.randint(TOP, size=T // 2); x, y = deal[r, s_].copy(), deal[r, t_].copy()
        ok = ~((deal[:, s_] == y).any(0) | (deal[:, t_] == x).any(0)); deal[r[ok], s_[ok]] = y[ok]; deal[r[ok], t_[ok]] = x[ok]
    order = np.lexsort((np.random.rand(TOP * T), deal.reshape(-1)))
    slot_token = order % T; pos = np.empty(TOP * T, np.int64); pos[order] = np.arange(TOP * T); pos = pos.reshape(TOP, T)
    g = np.random.uniform(0.5, 1.5, (TOP, T)); g = g / g.sum(0)
    w1 = [pack_weight(m, "e2m1") for m in n((E, K, H)) / np.sqrt(K) / s[None] * u[None, None, :]]
    w2 = [pack_weight(m, "e2m1") for m in n((E, H, N)) / np.sqrt(H) / u[None, :, None]]
    x = pack_weight(n((K, T)) * s, "e4m3")
    return {
        "x_words": x[0],
        "x_scales": x[1],
        "w1_words": np.stack([m[0] for m in w1]),
        "w1_scales": np.stack([m[1] for m in w1]),
        "w2_words": np.stack([m[0] for m in w2]),
        "w2_scales": np.stack([m[1] for m in w2]),
        "gate": np.stack([np.tile(r, (N, 1)) for r in g]).astype(np.float32),
        "offs": striped(slot_token),
        "pos1": striped(pos[0]),
        "pos2": striped(pos[1]),
        "pos3": striped(pos[2]),
    }


def reference(x_words, x_scales, w1_words, w1_scales, w2_words, w2_scales, gate, offs, pos1, pos2, pos3):
    idx = unstriped(offs)
    w1 = np.stack([unpack_weight(w1_words[e], w1_scales[e], "e2m1") for e in range(E)])
    w2 = np.stack([unpack_weight(w2_words[e], w2_scales[e], "e2m1") for e in range(E)])
    xq = unpack_weight(x_words, x_scales, "e4m3")[:, idx]
    h = gelu(by_expert(w1, xq))
    y = by_expert(w2, mxq(h, 0, "e4m3"))
    return sum(f64(gate[r]) * y[:, unstriped(p)] for r, p in enumerate((pos1, pos2, pos3)))

@@ -1,0 +1,198 @@
+from contextlib import ExitStack
+
+import concourse.mybir as mybir
+from concourse.masks import make_identity
+
+F32 = mybir.dt.float32
+BF16 = mybir.dt.bfloat16
+I32 = mybir.dt.int32
+U32 = mybir.dt.uint32
+U16 = mybir.dt.uint16
+U8 = mybir.dt.uint8
+FP8X4 = mybir.dt.float8_e4m3fn_x4
+FP4X4 = mybir.dt.float4_e2m1fn_x4
+GELU = mybir.ActivationFunctionType.Gelu_apprx_tanh
+MULT = mybir.AluOpType.mult
+ADD = mybir.AluOpType.add
+
+P = 128
+T, E, C, H, N = 512, 12, 128, 512, 128
+PASSES = 2
+SLOTS = E * C
+LIST_COLS = C // 16
+
+FLOPS = 2 * SLOTS * (1024 * H + H * N)
+
+GATHER_RUNS = [(0, 1), (1, 2), (2, 4), (4, 7), (7, 10), (10, 11), (11, 12)]
+W1_LOADS = [[(0, 1), (1, 2), (2, 4)], [(4, 6), (6, 8), (8, 10), (10, 12)]]
+EARLY = 4
+LEAD = 64
+H_GROUPS = [(0, 2), (2, 4), (4, 6), (6, 8), (8, 10), (10, 11), (11, 12)]
+Q_GROUPS = [(0, 4), (4, 8), (8, 10), (10, 11), (11, 12)]
+Y_ON_VECTOR = (0, 11)
+
+
+def tile_moe_pkd_mlp_gelu_kernel(
+    tc, x_words, x_scales, w1_words, w1_scales, w2_words, w2_scales, gate, offs, pos1, pos2, pos3, out
+):
+    nc = tc.nc
+    with ExitStack() as ctx:
+        keep = ctx.enter_context(tc.tile_pool(name="keep", bufs=1))
+        work = ctx.enter_context(tc.tile_pool(name="work", bufs=3))
+        a_psum = ctx.enter_context(tc.psum_pool(name="a_psum", bufs=4))
+        t_psum = ctx.enter_context(tc.psum_pool(name="t_psum", bufs=2))
+        y_psum = ctx.enter_context(tc.psum_pool(name="y_psum", bufs=2))
+
+        slot_list = keep.tile([P, E * LIST_COLS], U16, name="slot_list")
+        pos_lists = [keep.tile([P, T // 16], U16, name="pos%d" % r) for r in range(3)]
+        xw = [keep.tile([P, T], I32, name="xw%d" % o, align_bytes=64) for o in range(PASSES)]
+        xs = keep.tile([P, PASSES, T], U8, name="xs", align_bytes=64)
+        w1_early = keep.tile([P, EARLY * PASSES, 3 * H], U8, name="w1_early", tag="early", align_bytes=64)
+        w1_late = keep.tile([P, (E - EARLY) * PASSES, 3 * H], U8, name="w1_late", align_bytes=64)
+        w2 = keep.tile([P, E, 3 * N], U8, name="w2", align_bytes=64)
+        ident = keep.tile([P, P], F32, name="ident", align_bytes=64)
+        h_in = keep.tile([P, SLOTS, 4], BF16, name="h_in", align_bytes=64)
+        h_scales = keep.tile([P, SLOTS], U8, name="h_scales", align_bytes=64)
+        y_slots = keep.tile([P, SLOTS], F32, name="y_slots")
+        warm = keep.tile([P, 2], F32, name="warm")
+
+        def w1_records(e0, e1):
+            if e0 < EARLY:
+                return w1_early[:, e0 * PASSES : e1 * PASSES, :]
+            return w1_late[:, (e0 - EARLY) * PASSES : (e1 - EARLY) * PASSES, :]
+
+        def load_w1(loads):
+            e0, e1 = loads[0][0], loads[-1][1]
+            for q in range(4):
+                nc.sync.dma_start(
+                    out=w1_records(e0, e1)[32 * q : 32 * q + 4, :, :H].bitcast(I32),
+                    in_=w1_scales[e0:e1, :, 4 * q : 4 * q + 4, :].rearrange("e s r i -> r (e s) i").bitcast(I32),
+                )
+            for e0, e1 in loads:
+                nc.sync.dma_start(
+                    out=w1_records(e0, e1)[:, :, H:].bitcast(I32),
+                    in_=w1_words[e0:e1].rearrange("e s p b -> p (e s) b").bitcast(I32),
+                )
+
+        nc.gpsimd.memset(xs[:].rearrange("p o t -> p (o t)").bitcast(I32), 0)
+        nc.vector.memset(w1_early[:, :, : H + LEAD].bitcast(I32), 0)
+        nc.vector.memset(w1_late[:, :, : H + LEAD].bitcast(I32), 0)
+        nc.gpsimd.memset(warm[:, 0:1], 0.0)
+        nc.scalar.activation(warm[:, 1:2], warm[:, 0:1], GELU)
+        make_identity(nc, ident[:])
+        nc.gpsimd.memset(w2[:, :, : N + LEAD].bitcast(I32), 0)
+
+        nc.sync.dma_start(slot_list[:], offs)
+        for o in range(PASSES):
+            nc.sync.dma_start(out=xw[o][:], in_=x_words[o].rearrange("p t r -> p (t r)").bitcast(I32))
+        for q in range(4):
+            nc.sync.dma_start(
+                out=xs[32 * q : 32 * q + 4].bitcast(I32),
+                in_=x_scales[:, 4 * q : 4 * q + 4, :].rearrange("o r t -> r o t").bitcast(I32),
+            )
+        for loads in W1_LOADS:
+            load_w1(loads)
+        for q in range(4):
+            nc.sync.dma_start(
+                out=w2[32 * q : 32 * q + 4, :, :N].bitcast(I32),
+                in_=w2_scales[:, 0, 4 * q : 4 * q + 4, :].rearrange("e r n -> r e n").bitcast(I32),
+            )
+        nc.sync.dma_start(out=w2[:, :, N:].bitcast(I32), in_=w2_words[:, 0].rearrange("e p b -> p e b").bitcast(I32))
+        for lst, src in zip(pos_lists, (pos1, pos2, pos3)):
+            nc.sync.dma_start(lst[:], src)
+
+        tokens = {}
+
+        def gather(e0, e1):
+            entries = slot_list[:, e0 * LIST_COLS : e1 * LIST_COLS]
+            gw = work.tile([P, PASSES, (e1 - e0) * C], I32, name="gw", tag="gw", align_bytes=64)
+            gs = work.tile([P, PASSES, (e1 - e0) * C], U8, name="gs", tag="gs", align_bytes=64)
+            for o in range(PASSES):
+                nc.vector.tensor_copy(gw[:, o, :].bitcast(U32), xw[o][:].bitcast(U32).indirect(entries))
+            for o in range(PASSES):
+                nc.vector.tensor_copy(gs[:, o, :], xs[:, o, :].indirect(entries))
+            for e in range(e0, e1):
+                cols = slice((e - e0) * C, (e - e0 + 1) * C)
+                tokens[e] = [(gw[:, o, cols], gs[:, o, cols]) for o in range(PASSES)]
+
+        for run in GATHER_RUNS:
+            gather(*run)
+
+        h_rows = {}
+
+        def first_layer(e0, e1):
+            rows = work.tile([P, e1 - e0, H], BF16, name="h_rows", tag="h_rows", align_bytes=64)
+            h_rows[e0] = rows
+            for e in range(e0, e1):
+                a = a_psum.tile([P, H], F32, name="a")
+                for o in range(PASSES):
+                    nc.tensor.matmul_mx(
+                        out=a[:],
+                        lhsT=tokens[e][o][0].bitcast(FP8X4),
+                        lhsT_scale=tokens[e][o][1],
+                        rhs=w1_records(e, e + 1)[:, o, H:].bitcast(FP4X4),
+                        rhs_scale=w1_records(e, e + 1)[:, o, :H],
+                        start=(o == 0),
+                        stop=(o == PASSES - 1),
+                    )
+                nc.scalar.activation(
+                    rows[:, e - e0, :].rearrange("c (u p d) -> c u p d", u=2, d=2),
+                    a[:].rearrange("c (p u d) -> c u p d", u=2, d=2),
+                    GELU,
+                )
+
+        def turn(e0, e1):
+            turned = t_psum.tile([P, e1 - e0, 2, C], F32, name="turned", tag="turned")
+            for e in range(e0, e1):
+                words = h_rows[e0][:, e - e0, :].bitcast(F32)
+                for u in range(2):
+                    nc.tensor.transpose(turned[:, e - e0, u, :], words[:, u * P : (u + 1) * P], ident[:])
+            dst = h_in[:, e0 * C : e1 * C, :].rearrange("p c t -> p (c t)").bitcast(F32)
+            nc.scalar.copy(
+                dst.rearrange("p (e c u) -> p e c u", u=2, c=C),
+                turned[:].rearrange("p e u c -> p e c u"),
+            )
+
+        def second_layer(e0, e1):
+            cols = slice(e0 * C, e1 * C)
+            h_codes = work.tile([P, (e1 - e0) * C], U32, name="h_codes", tag="gw", align_bytes=64)
+            nc.vector.quantize_mx(
+                out=h_codes[:].bitcast(FP8X4),
+                scales=h_scales[:, cols],
+                in_=h_in[:, cols, :].rearrange("p c t -> p (c t)"),
+            )
+            y = y_psum.tile([P, (e1 - e0) * C], F32, name="y", tag="y")
+            for e in range(e0, e1):
+                own = slice((e - e0) * C, (e - e0 + 1) * C)
+                nc.tensor.matmul_mx(
+                    out=y[:, own],
+                    lhsT=w2[:, e, N:].bitcast(FP4X4),
+                    lhsT_scale=w2[:, e, :N],
+                    rhs=h_codes[:, own].bitcast(FP8X4),
+                    rhs_scale=h_scales[:, e * C : (e + 1) * C],
+                    start=True,
+                    stop=True,
+                )
+            if e0 in Y_ON_VECTOR:
+                nc.vector.tensor_copy(y_slots[:, cols], y[:])
+            else:
+                nc.scalar.copy(y_slots[:, cols], y[:])
+
+        first_layer(*H_GROUPS[0])
+        for g in range(1, len(H_GROUPS)):
+            first_layer(*H_GROUPS[g])
+            turn(*H_GROUPS[g - 1])
+        turn(*H_GROUPS[-1])
+        gates = keep.tile([P, 3, T], F32, name="gates", tag="early", align_bytes=64)
+        nc.sync.dma_start(out=gates[:], in_=gate.rearrange("r n t -> n r t"))
+        for group in Q_GROUPS:
+            second_layer(*group)
+
+        parts = [keep.tile([P, T], F32, name="part%d" % r) for r in range(3)]
+        pair = keep.tile([P, T], F32, name="pair")
+        total = keep.tile([P, T], F32, name="total")
+        for r in range(3):
+            nc.vector.tensor_tensor(parts[r][:], y_slots[:].indirect(pos_lists[r][:]), gates[:, r, :], MULT)
+        nc.vector.tensor_tensor(pair[:], parts[0][:], parts[1][:], ADD)
+        nc.vector.tensor_tensor(total[:], pair[:], parts[2][:], ADD)
+        nc.sync.dma_start(out=out, in_=total[:])

@@ -24,7 +24,6 @@ LIST_COLS = C // 16
 FLOPS = 2 * SLOTS * (1024 * H + H * N)
 
 GATHER_RUNS = [(0, 1), (1, 2), (2, 4), (4, 7), (7, 10), (10, 11), (11, 12)]
-W1_LOADS = [[(0, 1), (1, 2), (2, 4)], [(4, 6), (6, 8), (8, 10), (10, 12)]]
 EARLY = 4
 LEAD = 64
 H_GROUPS = [(0, 2), (2, 4), (4, 6), (6, 8), (8, 10), (10, 11), (11, 12)]
@@ -47,8 +46,9 @@ def tile_moe_pkd_mlp_gelu_kernel(
         pos_lists = [keep.tile([P, T // 16], U16, name="pos%d" % r) for r in range(3)]
         xw = [keep.tile([P, T], I32, name="xw%d" % o, align_bytes=64) for o in range(PASSES)]
         xs = keep.tile([P, PASSES, T], U8, name="xs", align_bytes=64)
-        w1_early = keep.tile([P, EARLY * PASSES, 3 * H], U8, name="w1_early", tag="early", align_bytes=64)
-        w1_late = keep.tile([P, (E - EARLY) * PASSES, 3 * H], U8, name="w1_late", align_bytes=64)
+        w1_early = keep.tile([P, EARLY, PASSES, 3 * H], U8, name="w1_early", tag="early", align_bytes=64)
+        w1_late = keep.tile([P, E - EARLY, PASSES, 3 * H], U8, name="w1_late", align_bytes=64)
+        h_rows = keep.tile([P, E, H], BF16, name="h_rows", align_bytes=64)
         w2 = keep.tile([P, E, 3 * N], U8, name="w2", align_bytes=64)
         ident = keep.tile([P, P], F32, name="ident", align_bytes=64)
         h_in = keep.tile([P, SLOTS, 4], BF16, name="h_in", align_bytes=64)
@@ -57,45 +57,49 @@ def tile_moe_pkd_mlp_gelu_kernel(
         warm = keep.tile([P, 2], F32, name="warm")
 
         def w1_records(e0, e1):
-            if e0 < EARLY:
-                return w1_early[:, e0 * PASSES : e1 * PASSES, :]
-            return w1_late[:, (e0 - EARLY) * PASSES : (e1 - EARLY) * PASSES, :]
+            held = w1_early[:, e0:e1] if e0 < EARLY else w1_late[:, e0 - EARLY : e1 - EARLY]
+            return held.rearrange("p e s b -> p (e s) b")
 
-        def load_w1(loads):
-            e0, e1 = loads[0][0], loads[-1][1]
-            for q in range(4):
+        def load_w1_scales(e0, e1):
+            for r in range(4):
                 nc.sync.dma_start(
-                    out=w1_records(e0, e1)[32 * q : 32 * q + 4, :, :H].bitcast(I32),
-                    in_=w1_scales[e0:e1, :, 4 * q : 4 * q + 4, :].rearrange("e s r i -> r (e s) i").bitcast(I32),
+                    out=w1_records(e0, e1)[r:P:32, :, :H].bitcast(I32),
+                    in_=w1_scales[e0:e1, :, r:16:4, :].rearrange("e s q i -> q (e s) i").bitcast(I32),
                 )
-            for e0, e1 in loads:
-                nc.sync.dma_start(
-                    out=w1_records(e0, e1)[:, :, H:].bitcast(I32),
-                    in_=w1_words[e0:e1].rearrange("e s p b -> p (e s) b").bitcast(I32),
-                )
+
+        def load_w1_words(e0, e1):
+            nc.sync.dma_start(
+                out=w1_records(e0, e1)[:, :, H:].bitcast(I32),
+                in_=w1_words[e0:e1].rearrange("e s p b -> p (e s) b").bitcast(I32),
+            )
 
         nc.gpsimd.memset(xs[:].rearrange("p o t -> p (o t)").bitcast(I32), 0)
-        nc.vector.memset(w1_early[:, :, : H + LEAD].bitcast(I32), 0)
-        nc.vector.memset(w1_late[:, :, : H + LEAD].bitcast(I32), 0)
+        nc.vector.memset(w1_records(0, EARLY)[:, :, : H + LEAD].bitcast(I32), 0)
+        nc.vector.memset(w1_records(EARLY, 7)[:, :, : H + LEAD].bitcast(I32), 0)
         nc.gpsimd.memset(warm[:, 0:1], 0.0)
         nc.scalar.activation(warm[:, 1:2], warm[:, 0:1], GELU)
+        nc.gpsimd.memset(w1_records(7, E)[:, :, : H + LEAD].bitcast(I32), 0)
         make_identity(nc, ident[:])
         nc.gpsimd.memset(w2[:, :, : N + LEAD].bitcast(I32), 0)
 
         nc.sync.dma_start(slot_list[:], offs)
         for o in range(PASSES):
             nc.sync.dma_start(out=xw[o][:], in_=x_words[o].rearrange("p t r -> p (t r)").bitcast(I32))
-        for q in range(4):
+        for r in range(4):
             nc.sync.dma_start(
-                out=xs[32 * q : 32 * q + 4].bitcast(I32),
-                in_=x_scales[:, 4 * q : 4 * q + 4, :].rearrange("o r t -> r o t").bitcast(I32),
+                out=xs[r:P:32].bitcast(I32),
+                in_=x_scales[:, r:16:4, :].rearrange("o q t -> q o t").bitcast(I32),
             )
-        for loads in W1_LOADS:
-            load_w1(loads)
-        for q in range(4):
+        load_w1_words(0, 2)
+        load_w1_scales(0, EARLY)
+        load_w1_words(2, EARLY)
+        load_w1_scales(EARLY, E)
+        for e in range(EARLY, E, 2):
+            load_w1_words(e, e + 2)
+        for r in range(4):
             nc.sync.dma_start(
-                out=w2[32 * q : 32 * q + 4, :, :N].bitcast(I32),
-                in_=w2_scales[:, 0, 4 * q : 4 * q + 4, :].rearrange("e r n -> r e n").bitcast(I32),
+                out=w2[r:P:32, :, :N].bitcast(I32),
+                in_=w2_scales[:, 0, r:16:4, :].rearrange("e q n -> q e n").bitcast(I32),
             )
         nc.sync.dma_start(out=w2[:, :, N:].bitcast(I32), in_=w2_words[:, 0].rearrange("e p b -> p e b").bitcast(I32))
         for lst, src in zip(pos_lists, (pos1, pos2, pos3)):
@@ -118,11 +122,7 @@ def tile_moe_pkd_mlp_gelu_kernel(
         for run in GATHER_RUNS:
             gather(*run)
 
-        h_rows = {}
-
         def first_layer(e0, e1):
-            rows = work.tile([P, e1 - e0, H], BF16, name="h_rows", tag="h_rows", align_bytes=64)
-            h_rows[e0] = rows
             for e in range(e0, e1):
                 a = a_psum.tile([P, H], F32, name="a")
                 for o in range(PASSES):
@@ -136,7 +136,7 @@ def tile_moe_pkd_mlp_gelu_kernel(
                         stop=(o == PASSES - 1),
                     )
                 nc.scalar.activation(
-                    rows[:, e - e0, :].rearrange("c (u p d) -> c u p d", u=2, d=2),
+                    h_rows[:, e, :].rearrange("c (u p d) -> c u p d", u=2, d=2),
                     a[:].rearrange("c (p u d) -> c u p d", u=2, d=2),
                     GELU,
                 )
@@ -144,7 +144,7 @@ def tile_moe_pkd_mlp_gelu_kernel(
         def turn(e0, e1):
             turned = t_psum.tile([P, e1 - e0, 2, C], F32, name="turned", tag="turned")
             for e in range(e0, e1):
-                words = h_rows[e0][:, e - e0, :].bitcast(F32)
+                words = h_rows[:, e, :].bitcast(F32)
                 for u in range(2):
                     nc.tensor.transpose(turned[:, e - e0, u, :], words[:, u * P : (u + 1) * P], ident[:])
             dst = h_in[:, e0 * C : e1 * C, :].rearrange("p c t -> p (c t)").bitcast(F32)

@@ -23,12 +23,13 @@ LIST_COLS = C // 16
 
 FLOPS = 2 * SLOTS * (1024 * H + H * N)
 
-GATHER_RUNS = [(0, 1), (1, 2), (2, 4), (4, 7), (7, 10), (10, 11), (11, 12)]
+GATHER_RUNS = [(0, 1), (1, 3), (3, 6), (6, 8), (8, 10), (10, 11), (11, 12)]
 EARLY = 4
 LEAD = 64
 H_GROUPS = [(0, 2), (2, 4), (4, 6), (6, 8), (8, 10), (10, 11), (11, 12)]
 Q_GROUPS = [(0, 4), (4, 8), (8, 10), (10, 11), (11, 12)]
-Y_ON_VECTOR = (0, 11)
+Y_ON_VECTOR = (4, 11)
+TURN_ON_VECTOR = (10,)
 
 
 def tile_moe_pkd_mlp_gelu_kernel(
@@ -38,9 +39,9 @@ def tile_moe_pkd_mlp_gelu_kernel(
     with ExitStack() as ctx:
         keep = ctx.enter_context(tc.tile_pool(name="keep", bufs=1))
         work = ctx.enter_context(tc.tile_pool(name="work", bufs=3))
-        a_psum = ctx.enter_context(tc.psum_pool(name="a_psum", bufs=4))
+        a_psum = ctx.enter_context(tc.psum_pool(name="a_psum", bufs=3))
         t_psum = ctx.enter_context(tc.psum_pool(name="t_psum", bufs=2))
-        y_psum = ctx.enter_context(tc.psum_pool(name="y_psum", bufs=2))
+        y_psum = ctx.enter_context(tc.psum_pool(name="y_psum", bufs=3))
 
         slot_list = keep.tile([P, E * LIST_COLS], U16, name="slot_list")
         pos_lists = [keep.tile([P, T // 16], U16, name="pos%d" % r) for r in range(3)]
@@ -148,7 +149,8 @@ def tile_moe_pkd_mlp_gelu_kernel(
                 for u in range(2):
                     nc.tensor.transpose(turned[:, e - e0, u, :], words[:, u * P : (u + 1) * P], ident[:])
             dst = h_in[:, e0 * C : e1 * C, :].rearrange("p c t -> p (c t)").bitcast(F32)
-            nc.scalar.copy(
+            copy = nc.vector.tensor_copy if e0 in TURN_ON_VECTOR else nc.scalar.copy
+            copy(
                 dst.rearrange("p (e c u) -> p e c u", u=2, c=C),
                 turned[:].rearrange("p e u c -> p e c u"),
             )
@@ -188,11 +190,34 @@ def tile_moe_pkd_mlp_gelu_kernel(
         for group in Q_GROUPS:
             second_layer(*group)
 
-        parts = [keep.tile([P, T], F32, name="part%d" % r) for r in range(3)]
-        pair = keep.tile([P, T], F32, name="pair")
-        total = keep.tile([P, T], F32, name="total")
-        for r in range(3):
-            nc.vector.tensor_tensor(parts[r][:], y_slots[:].indirect(pos_lists[r][:]), gates[:, r, :], MULT)
-        nc.vector.tensor_tensor(pair[:], parts[0][:], parts[1][:], ADD)
-        nc.vector.tensor_tensor(total[:], pair[:], parts[2][:], ADD)
-        nc.sync.dma_start(out=out, in_=total[:])
+        half = T // 2
+        blocks = half // P
+        parts = [[keep.tile([P, half], F32, name="part%d_%d" % (k, r)) for r in range(3)] for k in range(2)]
+        for k in range(2):
+            for r in range(3):
+                entries = pos_lists[r][:, k * half // 16 : (k + 1) * half // 16]
+                nc.vector.tensor_tensor(
+                    parts[k][r][:], y_slots[:].indirect(entries), gates[:, r, k * half : (k + 1) * half], MULT
+                )
+
+        summed = t_psum.tile([P, blocks, P], F32, name="summed", tag="turned")
+        for b in range(blocks):
+            for r in range(3):
+                nc.tensor.matmul(
+                    summed[:, b, :], parts[0][r][:, b * P : (b + 1) * P], ident[:],
+                    start=(r == 0), stop=(r == 2), is_transpose=True,
+                )
+        by_token = keep.tile([P, blocks, P], F32, name="by_token")
+        nc.scalar.copy(by_token[:], summed[:])
+        back = t_psum.tile([P, blocks, P], F32, name="back", tag="turned")
+        for b in range(blocks):
+            nc.tensor.transpose(back[:, b, :], by_token[:, b, :], ident[:])
+        first = keep.tile([P, half], F32, name="first")
+        nc.scalar.copy(first[:], back[:].rearrange("p b t -> p (b t)"))
+        nc.scalar.dma_start(out=out[:, :half], in_=first[:])
+
+        pair = keep.tile([P, half], F32, name="pair")
+        second = keep.tile([P, half], F32, name="second")
+        nc.vector.tensor_tensor(pair[:], parts[1][0][:], parts[1][1][:], ADD)
+        nc.vector.tensor_tensor(second[:], pair[:], parts[1][2][:], ADD)
+        nc.sync.dma_start(out=out[:, half:], in_=second[:])

@@ -20,16 +20,22 @@ T, E, C, H, N = 512, 12, 128, 512, 128
 PASSES = 2
 SLOTS = E * C
 LIST_COLS = C // 16
+LIVE = 112
+SHIFT = 16
+WINDOW = 1024
 
 FLOPS = 2 * SLOTS * (1024 * H + H * N)
 
-GATHER_RUNS = [(0, 1), (1, 3), (3, 6), (6, 8), (8, 10), (10, 11), (11, 12)]
-EARLY = 4
-LEAD = 64
+SCALE_MOVES = [(0, 2), (2, 7), (7, 12)]
+WORD_RUNS = [(0, 2), (2, 4), (4, 6), (6, 8), (8, 10), (10, 12)]
+W1_WORD_LOADS = [(0, 2), (2, 5), (5, 9), (9, 12)]
+W1_SCALE_LOADS = [(0, 2), (2, 5), (5, 9), (9, 12)]
+A_BANKS = 5
+T_BANKS = 3
 H_GROUPS = [(0, 2), (2, 4), (4, 6), (6, 8), (8, 10), (10, 11), (11, 12)]
 Q_GROUPS = [(0, 4), (4, 8), (8, 10), (10, 11), (11, 12)]
 Y_ON_VECTOR = (4, 11)
-TURN_ON_VECTOR = (10,)
+TURN_ON_VECTOR = (8, 10)
 
 
 def tile_moe_pkd_mlp_gelu_kernel(
@@ -38,140 +44,193 @@ def tile_moe_pkd_mlp_gelu_kernel(
     nc = tc.nc
     with ExitStack() as ctx:
         keep = ctx.enter_context(tc.tile_pool(name="keep", bufs=1))
-        work = ctx.enter_context(tc.tile_pool(name="work", bufs=3))
-        a_psum = ctx.enter_context(tc.psum_pool(name="a_psum", bufs=3))
-        t_psum = ctx.enter_context(tc.psum_pool(name="t_psum", bufs=2))
-        y_psum = ctx.enter_context(tc.psum_pool(name="y_psum", bufs=3))
+        banks = ctx.enter_context(tc.psum_pool(name="banks", bufs=1))
 
         slot_list = keep.tile([P, E * LIST_COLS], U16, name="slot_list")
         pos_lists = [keep.tile([P, T // 16], U16, name="pos%d" % r) for r in range(3)]
-        xw = [keep.tile([P, T], I32, name="xw%d" % o, align_bytes=64) for o in range(PASSES)]
-        xs = keep.tile([P, PASSES, T], U8, name="xs", align_bytes=64)
-        w1_early = keep.tile([P, EARLY, PASSES, 3 * H], U8, name="w1_early", tag="early", align_bytes=64)
-        w1_late = keep.tile([P, E - EARLY, PASSES, 3 * H], U8, name="w1_late", align_bytes=64)
-        h_rows = keep.tile([P, E, H], BF16, name="h_rows", align_bytes=64)
-        w2 = keep.tile([P, E, 3 * N], U8, name="w2", align_bytes=64)
+        xw = keep.tile([P, PASSES, T], I32, name="xw", align_bytes=64)
+        xs = keep.tile([P, WINDOW], U8, name="xs", align_bytes=64)
+        w1w = {
+            e0: keep.tile([P, (e1 - e0) * PASSES, 2 * H], U8, name="w1w%d" % e0, align_bytes=64)
+            for e0, e1 in W1_WORD_LOADS
+        }
+        w1s = {
+            e0: keep.tile([P, (e1 - e0) * PASSES, H], U8, name="w1s%d" % e0, align_bytes=64)
+            for e0, e1 in W1_SCALE_LOADS
+        }
+        h_rows = [keep.tile([P, H], BF16, name="h_rows%d" % e, align_bytes=64) for e in range(E)]
+        w2w = keep.tile([P, E, 2 * N], U8, name="w2w", align_bytes=64)
+        w2s = keep.tile([P, E, N], U8, name="w2s", align_bytes=64)
         ident = keep.tile([P, P], F32, name="ident", align_bytes=64)
-        h_in = keep.tile([P, SLOTS, 4], BF16, name="h_in", align_bytes=64)
+        h_in = {
+            e0: keep.tile([P, (e1 - e0) * H], BF16, name="h_in%d" % e0, align_bytes=64) for e0, e1 in Q_GROUPS
+        }
+        h_codes = keep.tile([P, SLOTS], U32, name="h_codes", align_bytes=64)
         h_scales = keep.tile([P, SLOTS], U8, name="h_scales", align_bytes=64)
         y_slots = keep.tile([P, SLOTS], F32, name="y_slots")
         warm = keep.tile([P, 2], F32, name="warm")
 
-        def w1_records(e0, e1):
-            held = w1_early[:, e0:e1] if e0 < EARLY else w1_late[:, e0 - EARLY : e1 - EARLY]
-            return held.rearrange("p e s b -> p (e s) b")
+        def record(tiles, loads, e, o):
+            e0 = max(a for a, b in loads if a <= e)
+            return tiles[e0][:, (e - e0) * PASSES + o, :]
 
         def load_w1_scales(e0, e1):
             for r in range(4):
                 nc.sync.dma_start(
-                    out=w1_records(e0, e1)[r:P:32, :, :H].bitcast(I32),
+                    out=w1s[e0][r:P:32].bitcast(I32),
                     in_=w1_scales[e0:e1, :, r:16:4, :].rearrange("e s q i -> q (e s) i").bitcast(I32),
                 )
 
         def load_w1_words(e0, e1):
             nc.sync.dma_start(
-                out=w1_records(e0, e1)[:, :, H:].bitcast(I32),
+                out=w1w[e0][:].bitcast(I32),
                 in_=w1_words[e0:e1].rearrange("e s p b -> p (e s) b").bitcast(I32),
             )
 
-        nc.gpsimd.memset(xs[:].rearrange("p o t -> p (o t)").bitcast(I32), 0)
-        nc.vector.memset(w1_records(0, EARLY)[:, :, : H + LEAD].bitcast(I32), 0)
-        nc.vector.memset(w1_records(EARLY, 7)[:, :, : H + LEAD].bitcast(I32), 0)
+        moved_tiles = {
+            e0: keep.tile([P, (e1 - e0) * C], U8, name="moved%d" % e0, align_bytes=64) for e0, e1 in SCALE_MOVES
+        }
+
+        def zero(engine, tile):
+            engine.memset(tile.bitcast(I32), 0)
+
+        def flat(tile):
+            return tile[:].rearrange("p a b -> p (a b)")
+
+        def load_x_scales():
+            for r in range(4):
+                nc.sync.dma_start(
+                    out=xs[r:P:SHIFT, :T].bitcast(I32),
+                    in_=x_scales[:, r:16:4, :].rearrange("o q t -> q o t").bitcast(I32),
+                )
+
+        def load_x_words():
+            nc.sync.dma_start(out=xw[:], in_=x_words.rearrange("o p t r -> p o (t r)").bitcast(I32))
+
+        def load_w2_scales():
+            for r in range(4):
+                nc.sync.dma_start(
+                    out=w2s[r:P:32].bitcast(I32),
+                    in_=w2_scales[:, 0, r:16:4, :].rearrange("e q n -> q e n").bitcast(I32),
+                )
+
+        def load_w2_words():
+            nc.sync.dma_start(out=w2w[:].bitcast(I32), in_=w2_words[:, 0].rearrange("e p b -> p e b").bitcast(I32))
+
+        token_words = {}
+        token_scales = {}
+
+        def entries(e0, e1):
+            return slot_list[:, e0 * LIST_COLS : e1 * LIST_COLS]
+
+        def gather_scales(e0, e1, queue):
+            both = keep.tile([P, (e1 - e0) * C], U8, name="both%d" % e0, tag="both", bufs=2, align_bytes=64)
+            moved = moved_tiles[e0]
+            nc.vector.tensor_copy(both[:], xs[:].indirect(entries(e0, e1)))
+            queue.dma_start(out=moved[:LIVE].bitcast(I32), in_=both[SHIFT : LIVE + SHIFT].bitcast(I32))
+            for e in range(e0, e1):
+                cols = slice((e - e0) * C, (e - e0 + 1) * C)
+                token_scales[e] = [both[:, cols], moved[:, cols]]
+
+        def gather_words(e0, e1):
+            gw = keep.tile([P, PASSES, (e1 - e0) * C], I32, name="gw%d" % e0, tag="gw", bufs=3, align_bytes=64)
+            step = 1 if e0 == 0 else e1 - e0
+            for a in range(e0, e1, step):
+                cols = slice((a - e0) * C, (a + step - e0) * C)
+                for o in range(PASSES):
+                    nc.vector.tensor_copy(
+                        gw[:, o, cols].bitcast(U32), xw[:, o, :].bitcast(U32).indirect(entries(a, a + step))
+                    )
+            for e in range(e0, e1):
+                cols = slice((e - e0) * C, (e - e0 + 1) * C)
+                token_words[e] = [gw[:, o, cols] for o in range(PASSES)]
+
+        zero(nc.gpsimd, xs[:])
+        zero(nc.vector, flat(w1s[0]))
+        zero(nc.vector, flat(w1s[2]))
+        for e0, e1 in SCALE_MOVES[:2]:
+            zero(nc.vector, moved_tiles[e0][:])
+        zero(nc.vector, flat(w1s[5]))
         nc.gpsimd.memset(warm[:, 0:1], 0.0)
         nc.scalar.activation(warm[:, 1:2], warm[:, 0:1], GELU)
-        nc.gpsimd.memset(w1_records(7, E)[:, :, : H + LEAD].bitcast(I32), 0)
         make_identity(nc, ident[:])
-        nc.gpsimd.memset(w2[:, :, : N + LEAD].bitcast(I32), 0)
-
+        load_x_scales()
         nc.sync.dma_start(slot_list[:], offs)
-        for o in range(PASSES):
-            nc.sync.dma_start(out=xw[o][:], in_=x_words[o].rearrange("p t r -> p (t r)").bitcast(I32))
-        for r in range(4):
-            nc.sync.dma_start(
-                out=xs[r:P:32].bitcast(I32),
-                in_=x_scales[:, r:16:4, :].rearrange("o q t -> q o t").bitcast(I32),
-            )
+        load_x_words()
         load_w1_words(0, 2)
-        load_w1_scales(0, EARLY)
-        load_w1_words(2, EARLY)
-        load_w1_scales(EARLY, E)
-        for e in range(EARLY, E, 2):
-            load_w1_words(e, e + 2)
-        for r in range(4):
-            nc.sync.dma_start(
-                out=w2[r:P:32, :, :N].bitcast(I32),
-                in_=w2_scales[:, 0, r:16:4, :].rearrange("e q n -> q e n").bitcast(I32),
-            )
-        nc.sync.dma_start(out=w2[:, :, N:].bitcast(I32), in_=w2_words[:, 0].rearrange("e p b -> p e b").bitcast(I32))
+        load_w1_scales(0, 2)
+        gather_scales(*SCALE_MOVES[0], nc.scalar)
+        load_w1_words(2, 5)
+        load_w1_scales(2, 5)
+        gather_scales(*SCALE_MOVES[1], nc.scalar)
+        zero(nc.vector, flat(w1s[9]))
+        zero(nc.vector, moved_tiles[SCALE_MOVES[2][0]][:])
+        zero(nc.vector, flat(w2s))
+        for run in WORD_RUNS[:3]:
+            gather_words(*run)
+        load_w1_words(5, 9)
+        load_w1_scales(5, 9)
+        gather_scales(*SCALE_MOVES[2], nc.sync)
+        for run in WORD_RUNS[3:]:
+            gather_words(*run)
+        load_w1_words(9, 12)
+        load_w1_scales(9, 12)
+        load_w2_words()
+        load_w2_scales()
         for lst, src in zip(pos_lists, (pos1, pos2, pos3)):
             nc.sync.dma_start(lst[:], src)
 
-        tokens = {}
-
-        def gather(e0, e1):
-            entries = slot_list[:, e0 * LIST_COLS : e1 * LIST_COLS]
-            gw = work.tile([P, PASSES, (e1 - e0) * C], I32, name="gw", tag="gw", align_bytes=64)
-            gs = work.tile([P, PASSES, (e1 - e0) * C], U8, name="gs", tag="gs", align_bytes=64)
-            for o in range(PASSES):
-                nc.vector.tensor_copy(gw[:, o, :].bitcast(U32), xw[o][:].bitcast(U32).indirect(entries))
-            for o in range(PASSES):
-                nc.vector.tensor_copy(gs[:, o, :], xs[:, o, :].indirect(entries))
-            for e in range(e0, e1):
-                cols = slice((e - e0) * C, (e - e0 + 1) * C)
-                tokens[e] = [(gw[:, o, cols], gs[:, o, cols]) for o in range(PASSES)]
-
-        for run in GATHER_RUNS:
-            gather(*run)
-
         def first_layer(e0, e1):
             for e in range(e0, e1):
-                a = a_psum.tile([P, H], F32, name="a")
+                a = banks.tile([P, H], F32, name="a", tag="a%d" % (e % A_BANKS))
                 for o in range(PASSES):
                     nc.tensor.matmul_mx(
                         out=a[:],
-                        lhsT=tokens[e][o][0].bitcast(FP8X4),
-                        lhsT_scale=tokens[e][o][1],
-                        rhs=w1_records(e, e + 1)[:, o, H:].bitcast(FP4X4),
-                        rhs_scale=w1_records(e, e + 1)[:, o, :H],
+                        lhsT=token_words[e][o].bitcast(FP8X4),
+                        lhsT_scale=token_scales[e][o],
+                        rhs=record(w1w, W1_WORD_LOADS, e, o).bitcast(FP4X4),
+                        rhs_scale=record(w1s, W1_SCALE_LOADS, e, o),
                         start=(o == 0),
                         stop=(o == PASSES - 1),
                     )
                 nc.scalar.activation(
-                    h_rows[:, e, :].rearrange("c (u p d) -> c u p d", u=2, d=2),
+                    h_rows[e][:].rearrange("c (u p d) -> c u p d", u=2, d=2),
                     a[:].rearrange("c (p u d) -> c u p d", u=2, d=2),
                     GELU,
                 )
 
-        def turn(e0, e1):
-            turned = t_psum.tile([P, e1 - e0, 2, C], F32, name="turned", tag="turned")
+        def turn(g):
+            e0, e1 = H_GROUPS[g]
+            turned = banks.tile([P, e1 - e0, 2, C], F32, name="turned", tag="t%d" % (g % T_BANKS))
             for e in range(e0, e1):
-                words = h_rows[:, e, :].bitcast(F32)
+                words = h_rows[e][:].bitcast(F32)
                 for u in range(2):
                     nc.tensor.transpose(turned[:, e - e0, u, :], words[:, u * P : (u + 1) * P], ident[:])
-            dst = h_in[:, e0 * C : e1 * C, :].rearrange("p c t -> p (c t)").bitcast(F32)
+            q0 = max(a for a, b in Q_GROUPS if a <= e0)
+            dst = h_in[q0][:, (e0 - q0) * H : (e1 - q0) * H].bitcast(F32)
             copy = nc.vector.tensor_copy if e0 in TURN_ON_VECTOR else nc.scalar.copy
             copy(
                 dst.rearrange("p (e c u) -> p e c u", u=2, c=C),
                 turned[:].rearrange("p e u c -> p e c u"),
             )
 
-        def second_layer(e0, e1):
+        def second_layer(g):
+            e0, e1 = Q_GROUPS[g]
             cols = slice(e0 * C, e1 * C)
-            h_codes = work.tile([P, (e1 - e0) * C], U32, name="h_codes", tag="gw", align_bytes=64)
             nc.vector.quantize_mx(
-                out=h_codes[:].bitcast(FP8X4),
+                out=h_codes[:, cols].bitcast(FP8X4),
                 scales=h_scales[:, cols],
-                in_=h_in[:, cols, :].rearrange("p c t -> p (c t)"),
+                in_=h_in[e0][:],
             )
-            y = y_psum.tile([P, (e1 - e0) * C], F32, name="y", tag="y")
+            y = banks.tile([P, (e1 - e0) * C], F32, name="y", tag="a%d" % ((E + g) % A_BANKS))
             for e in range(e0, e1):
-                own = slice((e - e0) * C, (e - e0 + 1) * C)
+                own = slice(e * C, (e + 1) * C)
                 nc.tensor.matmul_mx(
-                    out=y[:, own],
-                    lhsT=w2[:, e, N:].bitcast(FP4X4),
-                    lhsT_scale=w2[:, e, :N],
+                    out=y[:, (e - e0) * C : (e - e0 + 1) * C],
+                    lhsT=w2w[:, e, :].bitcast(FP4X4),
+                    lhsT_scale=w2s[:, e, :],
                     rhs=h_codes[:, own].bitcast(FP8X4),
-                    rhs_scale=h_scales[:, e * C : (e + 1) * C],
+                    rhs_scale=h_scales[:, own],
                     start=True,
                     stop=True,
                 )
@@ -183,24 +242,24 @@ def tile_moe_pkd_mlp_gelu_kernel(
         first_layer(*H_GROUPS[0])
         for g in range(1, len(H_GROUPS)):
             first_layer(*H_GROUPS[g])
-            turn(*H_GROUPS[g - 1])
-        turn(*H_GROUPS[-1])
-        gates = keep.tile([P, 3, T], F32, name="gates", tag="early", align_bytes=64)
+            turn(g - 1)
+        turn(len(H_GROUPS) - 1)
+        gates = keep.tile([P, 3, T], F32, name="gates", align_bytes=64)
         nc.sync.dma_start(out=gates[:], in_=gate.rearrange("r n t -> n r t"))
-        for group in Q_GROUPS:
-            second_layer(*group)
+        for g in range(len(Q_GROUPS)):
+            second_layer(g)
 
         half = T // 2
         blocks = half // P
         parts = [[keep.tile([P, half], F32, name="part%d_%d" % (k, r)) for r in range(3)] for k in range(2)]
         for k in range(2):
             for r in range(3):
-                entries = pos_lists[r][:, k * half // 16 : (k + 1) * half // 16]
+                picks = pos_lists[r][:, k * half // 16 : (k + 1) * half // 16]
                 nc.vector.tensor_tensor(
-                    parts[k][r][:], y_slots[:].indirect(entries), gates[:, r, k * half : (k + 1) * half], MULT
+                    parts[k][r][:], y_slots[:].indirect(picks), gates[:, r, k * half : (k + 1) * half], MULT
                 )
 
-        summed = t_psum.tile([P, blocks, P], F32, name="summed", tag="turned")
+        summed = banks.tile([P, blocks, P], F32, name="summed", tag="t0")
         for b in range(blocks):
             for r in range(3):
                 nc.tensor.matmul(
@@ -209,7 +268,7 @@ def tile_moe_pkd_mlp_gelu_kernel(
                 )
         by_token = keep.tile([P, blocks, P], F32, name="by_token")
         nc.scalar.copy(by_token[:], summed[:])
-        back = t_psum.tile([P, blocks, P], F32, name="back", tag="turned")
+        back = banks.tile([P, blocks, P], F32, name="back", tag="t1")
         for b in range(blocks):
             nc.tensor.transpose(back[:, b, :], by_token[:, b, :], ident[:])
         first = keep.tile([P, half], F32, name="first")

@@ -30,8 +30,8 @@ SCALE_MOVES = [(0, 2), (2, 7), (7, 12)]
 WORD_RUNS = [(0, 2), (2, 4), (4, 6), (6, 8), (8, 10), (10, 12)]
 W1_WORD_LOADS = [(0, 2), (2, 5), (5, 9), (9, 12)]
 W1_SCALE_LOADS = [(0, 2), (2, 5), (5, 9), (9, 12)]
-A_BANKS = 5
-T_BANKS = 3
+TURN_BANKS = ["even1", "even2", "even0", "even1", "even2", "spare0", "spare1"]
+Y_BANKS = ["odd0", "even0", "odd1", "even1", "odd2"]
 H_GROUPS = [(0, 2), (2, 4), (4, 6), (6, 8), (8, 10), (10, 11), (11, 12)]
 Q_GROUPS = [(0, 4), (4, 8), (8, 10), (10, 11), (11, 12)]
 Y_ON_VECTOR = (4, 11)
@@ -60,7 +60,7 @@ def tile_moe_pkd_mlp_gelu_kernel(
         }
         h_rows = [keep.tile([P, H], BF16, name="h_rows%d" % e, align_bytes=64) for e in range(E)]
         w2w = keep.tile([P, E, 2 * N], U8, name="w2w", align_bytes=64)
-        w2s = keep.tile([P, E, N], U8, name="w2s", align_bytes=64)
+        w2s = w1s[0][:].rearrange("p a b -> p (a b)")[:, : E * N].rearrange("p (e n) -> p e n", n=N)
         ident = keep.tile([P, P], F32, name="ident", align_bytes=64)
         h_in = {
             e0: keep.tile([P, (e1 - e0) * H], BF16, name="h_in%d" % e0, align_bytes=64) for e0, e1 in Q_GROUPS
@@ -88,8 +88,9 @@ def tile_moe_pkd_mlp_gelu_kernel(
             )
 
         moved_tiles = {
-            e0: keep.tile([P, (e1 - e0) * C], U8, name="moved%d" % e0, align_bytes=64) for e0, e1 in SCALE_MOVES
+            e0: keep.tile([P, 5 * C], U8, name="moved%d" % e0, align_bytes=64) for e0, e1 in SCALE_MOVES[:2]
         }
+        moved_tiles[7] = moved_tiles[0]
 
         def zero(engine, tile):
             engine.memset(tile.bitcast(I32), 0)
@@ -125,7 +126,7 @@ def tile_moe_pkd_mlp_gelu_kernel(
 
         def gather_scales(e0, e1, queue):
             both = keep.tile([P, (e1 - e0) * C], U8, name="both%d" % e0, tag="both", bufs=2, align_bytes=64)
-            moved = moved_tiles[e0]
+            moved = moved_tiles[e0][:, : (e1 - e0) * C]
             nc.vector.tensor_copy(both[:], xs[:].indirect(entries(e0, e1)))
             queue.dma_start(out=moved[:LIVE].bitcast(I32), in_=both[SHIFT : LIVE + SHIFT].bitcast(I32))
             for e in range(e0, e1):
@@ -154,6 +155,7 @@ def tile_moe_pkd_mlp_gelu_kernel(
         nc.gpsimd.memset(warm[:, 0:1], 0.0)
         nc.scalar.activation(warm[:, 1:2], warm[:, 0:1], GELU)
         make_identity(nc, ident[:])
+        zero(nc.gpsimd, flat(w1s[9]))
         load_x_scales()
         nc.sync.dma_start(slot_list[:], offs)
         load_x_words()
@@ -163,26 +165,14 @@ def tile_moe_pkd_mlp_gelu_kernel(
         load_w1_words(2, 5)
         load_w1_scales(2, 5)
         gather_scales(*SCALE_MOVES[1], nc.scalar)
-        zero(nc.vector, flat(w1s[9]))
-        zero(nc.vector, moved_tiles[SCALE_MOVES[2][0]][:])
-        zero(nc.vector, flat(w2s))
         for run in WORD_RUNS[:3]:
             gather_words(*run)
         load_w1_words(5, 9)
         load_w1_scales(5, 9)
-        gather_scales(*SCALE_MOVES[2], nc.sync)
-        for run in WORD_RUNS[3:]:
-            gather_words(*run)
-        load_w1_words(9, 12)
-        load_w1_scales(9, 12)
-        load_w2_words()
-        load_w2_scales()
-        for lst, src in zip(pos_lists, (pos1, pos2, pos3)):
-            nc.sync.dma_start(lst[:], src)
 
         def first_layer(e0, e1):
             for e in range(e0, e1):
-                a = banks.tile([P, H], F32, name="a", tag="a%d" % (e % A_BANKS))
+                a = banks.tile([P, H], F32, name="a", tag=("even%d", "odd%d")[e % 2] % (e // 2 % 3))
                 for o in range(PASSES):
                     nc.tensor.matmul_mx(
                         out=a[:],
@@ -201,7 +191,7 @@ def tile_moe_pkd_mlp_gelu_kernel(
 
         def turn(g):
             e0, e1 = H_GROUPS[g]
-            turned = banks.tile([P, e1 - e0, 2, C], F32, name="turned", tag="t%d" % (g % T_BANKS))
+            turned = banks.tile([P, e1 - e0, 2, C], F32, name="turned", tag=TURN_BANKS[g])
             for e in range(e0, e1):
                 words = h_rows[e][:].bitcast(F32)
                 for u in range(2):
@@ -222,7 +212,7 @@ def tile_moe_pkd_mlp_gelu_kernel(
                 scales=h_scales[:, cols],
                 in_=h_in[e0][:],
             )
-            y = banks.tile([P, (e1 - e0) * C], F32, name="y", tag="a%d" % ((E + g) % A_BANKS))
+            y = banks.tile([P, (e1 - e0) * C], F32, name="y", tag=Y_BANKS[g])
             for e in range(e0, e1):
                 own = slice(e * C, (e + 1) * C)
                 nc.tensor.matmul_mx(
@@ -240,6 +230,15 @@ def tile_moe_pkd_mlp_gelu_kernel(
                 nc.scalar.copy(y_slots[:, cols], y[:])
 
         first_layer(*H_GROUPS[0])
+        gather_scales(*SCALE_MOVES[2], nc.sync)
+        for run in WORD_RUNS[3:]:
+            gather_words(*run)
+        load_w1_words(9, 12)
+        load_w1_scales(9, 12)
+        load_w2_words()
+        load_w2_scales()
+        for lst, src in zip(pos_lists, (pos1, pos2, pos3)):
+            nc.sync.dma_start(lst[:], src)
         for g in range(1, len(H_GROUPS)):
             first_layer(*H_GROUPS[g])
             turn(g - 1)
@@ -259,7 +258,7 @@ def tile_moe_pkd_mlp_gelu_kernel(
                     parts[k][r][:], y_slots[:].indirect(picks), gates[:, r, k * half : (k + 1) * half], MULT
                 )
 
-        summed = banks.tile([P, blocks, P], F32, name="summed", tag="t0")
+        summed = banks.tile([P, blocks, P], F32, name="summed", tag="spare0")
         for b in range(blocks):
             for r in range(3):
                 nc.tensor.matmul(
@@ -268,7 +267,7 @@ def tile_moe_pkd_mlp_gelu_kernel(
                 )
         by_token = keep.tile([P, blocks, P], F32, name="by_token")
         nc.scalar.copy(by_token[:], summed[:])
-        back = banks.tile([P, blocks, P], F32, name="back", tag="t1")
+        back = banks.tile([P, blocks, P], F32, name="back", tag="spare1")
         for b in range(blocks):
             nc.tensor.transpose(back[:, b, :], by_token[:, b, :], ident[:])
         first = keep.tile([P, half], F32, name="first")

@@ -68,7 +68,6 @@ def tile_moe_pkd_mlp_gelu_kernel(
         h_codes = keep.tile([P, SLOTS], U32, name="h_codes", align_bytes=64)
         h_scales = keep.tile([P, SLOTS], U8, name="h_scales", align_bytes=64)
         y_slots = keep.tile([P, SLOTS], F32, name="y_slots")
-        warm = keep.tile([P, 2], F32, name="warm")
 
         def record(tiles, loads, e, o):
             e0 = max(a for a, b in loads if a <= e)
@@ -152,8 +151,6 @@ def tile_moe_pkd_mlp_gelu_kernel(
         for e0, e1 in SCALE_MOVES[:2]:
             zero(nc.vector, moved_tiles[e0][:])
         zero(nc.vector, flat(w1s[5]))
-        nc.gpsimd.memset(warm[:, 0:1], 0.0)
-        nc.scalar.activation(warm[:, 1:2], warm[:, 0:1], GELU)
         make_identity(nc, ident[:])
         zero(nc.gpsimd, flat(w1s[9]))
         load_x_scales()

@@ -27,15 +27,17 @@ WINDOW = 1024
 FLOPS = 2 * SLOTS * (1024 * H + H * N)
 
 SCALE_MOVES = [(0, 2), (2, 7), (7, 12)]
-WORD_RUNS = [(0, 2), (2, 4), (4, 6), (6, 8), (8, 10), (10, 12)]
-W1_WORD_LOADS = [(0, 2), (2, 5), (5, 9), (9, 12)]
-W1_SCALE_LOADS = [(0, 2), (2, 5), (5, 9), (9, 12)]
-TURN_BANKS = ["even1", "even2", "even0", "even1", "even2", "spare0", "spare1"]
-Y_BANKS = ["odd0", "even0", "odd1", "even1", "odd2"]
+WORD_RUNS = [(0, 1), (1, 2), (2, 4), (4, 6), (6, 8), (8, 10), (10, 12)]
+W1_WORD_LOADS = [(0, 2), (2, 4), (4, 6), (6, 8), (8, 10), (10, 12)]
+W1_SCALE_LOADS = [(0, 4), (4, 8), (8, 12)]
+W2_WORD_LOADS = [(0, 6), (6, 12)]
 H_GROUPS = [(0, 2), (2, 4), (4, 6), (6, 8), (8, 10), (10, 11), (11, 12)]
-Q_GROUPS = [(0, 4), (4, 8), (8, 10), (10, 11), (11, 12)]
-Y_ON_VECTOR = (4, 11)
-TURN_ON_VECTOR = (8, 10)
+A_BANKS = ["b0", "b1", "b2", "b3", "b4", "b5", "b6", "b7", "b0", "b1", "b3", "b6"]
+TURN_BANKS = ["b2", "b4", "b5", "b0", "b7", "b1", "b2"]
+Q_GROUPS = [(0, 4), (4, 6), (6, 8), (8, 10), (10, 11), (11, 12)]
+Y_BANKS = ["b4", "b5", "b3", "b6", "b0", "b7"]
+Y_ON_VECTOR = (11,)
+TURN_ON_VECTOR = (4, 6, 10)
 
 
 def tile_moe_pkd_mlp_gelu_kernel(
@@ -48,7 +50,7 @@ def tile_moe_pkd_mlp_gelu_kernel(
 
         slot_list = keep.tile([P, E * LIST_COLS], U16, name="slot_list")
         pos_lists = [keep.tile([P, T // 16], U16, name="pos%d" % r) for r in range(3)]
-        xw = keep.tile([P, PASSES, T], I32, name="xw", align_bytes=64)
+        xw = [keep.tile([P, T], I32, name="xw%d" % o, align_bytes=64) for o in range(PASSES)]
         xs = keep.tile([P, WINDOW], U8, name="xs", align_bytes=64)
         w1w = {
             e0: keep.tile([P, (e1 - e0) * PASSES, 2 * H], U8, name="w1w%d" % e0, align_bytes=64)
@@ -59,8 +61,10 @@ def tile_moe_pkd_mlp_gelu_kernel(
             for e0, e1 in W1_SCALE_LOADS
         }
         h_rows = [keep.tile([P, H], BF16, name="h_rows%d" % e, align_bytes=64) for e in range(E)]
-        w2w = keep.tile([P, E, 2 * N], U8, name="w2w", align_bytes=64)
-        w2s = w1s[0][:].rearrange("p a b -> p (a b)")[:, : E * N].rearrange("p (e n) -> p e n", n=N)
+        w2w = {
+            e0: keep.tile([P, e1 - e0, 2 * N], U8, name="w2w%d" % e0, align_bytes=64) for e0, e1 in W2_WORD_LOADS
+        }
+        w2s = keep.tile([P, E, N], U8, name="w2s", align_bytes=64)
         ident = keep.tile([P, P], F32, name="ident", align_bytes=64)
         h_in = {
             e0: keep.tile([P, (e1 - e0) * H], BF16, name="h_in%d" % e0, align_bytes=64) for e0, e1 in Q_GROUPS
@@ -68,9 +72,19 @@ def tile_moe_pkd_mlp_gelu_kernel(
         h_codes = keep.tile([P, SLOTS], U32, name="h_codes", align_bytes=64)
         h_scales = keep.tile([P, SLOTS], U8, name="h_scales", align_bytes=64)
         y_slots = keep.tile([P, SLOTS], F32, name="y_slots")
+        gates = keep.tile([P, 3, T], F32, name="gates", align_bytes=64)
+        both = {
+            e0: keep.tile([P, (e1 - e0) * C], U8, name="both%d" % e0, align_bytes=64) for e0, e1 in SCALE_MOVES
+        }
+        moved = {
+            e0: keep.tile([P, (e1 - e0) * C], U8, name="moved%d" % e0, align_bytes=64) for e0, e1 in SCALE_MOVES
+        }
+
+        def first_of(groups, e):
+            return max(a for a, b in groups if a <= e)
 
         def record(tiles, loads, e, o):
-            e0 = max(a for a, b in loads if a <= e)
+            e0 = first_of(loads, e)
             return tiles[e0][:, (e - e0) * PASSES + o, :]
 
         def load_w1_scales(e0, e1):
@@ -86,11 +100,6 @@ def tile_moe_pkd_mlp_gelu_kernel(
                 in_=w1_words[e0:e1].rearrange("e s p b -> p (e s) b").bitcast(I32),
             )
 
-        moved_tiles = {
-            e0: keep.tile([P, 5 * C], U8, name="moved%d" % e0, align_bytes=64) for e0, e1 in SCALE_MOVES[:2]
-        }
-        moved_tiles[7] = moved_tiles[0]
-
         def zero(engine, tile):
             engine.memset(tile.bitcast(I32), 0)
 
@@ -104,8 +113,8 @@ def tile_moe_pkd_mlp_gelu_kernel(
                     in_=x_scales[:, r:16:4, :].rearrange("o q t -> q o t").bitcast(I32),
                 )
 
-        def load_x_words():
-            nc.sync.dma_start(out=xw[:], in_=x_words.rearrange("o p t r -> p o (t r)").bitcast(I32))
+        def load_x_words(o):
+            nc.sync.dma_start(out=xw[o][:], in_=x_words[o].rearrange("p t r -> p (t r)").bitcast(I32))
 
         def load_w2_scales():
             for r in range(4):
@@ -114,77 +123,90 @@ def tile_moe_pkd_mlp_gelu_kernel(
                     in_=w2_scales[:, 0, r:16:4, :].rearrange("e q n -> q e n").bitcast(I32),
                 )
 
-        def load_w2_words():
-            nc.sync.dma_start(out=w2w[:].bitcast(I32), in_=w2_words[:, 0].rearrange("e p b -> p e b").bitcast(I32))
+        def load_w2_words(e0, e1):
+            nc.sync.dma_start(
+                out=w2w[e0][:].bitcast(I32), in_=w2_words[e0:e1, 0].rearrange("e p b -> p e b").bitcast(I32)
+            )
 
         token_words = {}
-        token_scales = {}
 
         def entries(e0, e1):
             return slot_list[:, e0 * LIST_COLS : e1 * LIST_COLS]
 
-        def gather_scales(e0, e1, queue):
-            both = keep.tile([P, (e1 - e0) * C], U8, name="both%d" % e0, tag="both", bufs=2, align_bytes=64)
-            moved = moved_tiles[e0][:, : (e1 - e0) * C]
-            nc.vector.tensor_copy(both[:], xs[:].indirect(entries(e0, e1)))
-            queue.dma_start(out=moved[:LIVE].bitcast(I32), in_=both[SHIFT : LIVE + SHIFT].bitcast(I32))
-            for e in range(e0, e1):
-                cols = slice((e - e0) * C, (e - e0 + 1) * C)
-                token_scales[e] = [both[:, cols], moved[:, cols]]
+        def gather_scales(e0, e1):
+            nc.vector.tensor_copy(both[e0][:], xs[:].indirect(entries(e0, e1)))
+
+        def move_scales(e0, queue):
+            queue.dma_start(out=moved[e0][:LIVE].bitcast(I32), in_=both[e0][SHIFT : LIVE + SHIFT].bitcast(I32))
+
+        def token_scales(e, o):
+            e0 = first_of(SCALE_MOVES, e)
+            return (both, moved)[o][e0][:, (e - e0) * C : (e - e0 + 1) * C]
 
         def gather_words(e0, e1):
-            gw = keep.tile([P, PASSES, (e1 - e0) * C], I32, name="gw%d" % e0, tag="gw", bufs=3, align_bytes=64)
-            step = 1 if e0 == 0 else e1 - e0
-            for a in range(e0, e1, step):
-                cols = slice((a - e0) * C, (a + step - e0) * C)
-                for o in range(PASSES):
-                    nc.vector.tensor_copy(
-                        gw[:, o, cols].bitcast(U32), xw[:, o, :].bitcast(U32).indirect(entries(a, a + step))
-                    )
+            gw = keep.tile([P, PASSES, (e1 - e0) * C], I32, name="gw%d" % e0, align_bytes=64)
+            for o in range(PASSES):
+                nc.vector.tensor_copy(gw[:, o, :].bitcast(U32), xw[o][:].bitcast(U32).indirect(entries(e0, e1)))
             for e in range(e0, e1):
                 cols = slice((e - e0) * C, (e - e0 + 1) * C)
                 token_words[e] = [gw[:, o, cols] for o in range(PASSES)]
 
         zero(nc.gpsimd, xs[:])
-        zero(nc.vector, flat(w1s[0]))
-        zero(nc.vector, flat(w1s[2]))
-        for e0, e1 in SCALE_MOVES[:2]:
-            zero(nc.vector, moved_tiles[e0][:])
-        zero(nc.vector, flat(w1s[5]))
+        zero(nc.gpsimd, flat(w1s[0])[:, : 4 * H])
+        zero(nc.vector, flat(w1s[0])[:, 4 * H :])
+        zero(nc.vector, moved[0][:])
+        zero(nc.vector, moved[2][:])
+        zero(nc.vector, flat(w1s[4]))
+        zero(nc.gpsimd, flat(w1s[8]))
+        zero(nc.gpsimd, moved[7][:])
         make_identity(nc, ident[:])
-        zero(nc.gpsimd, flat(w1s[9]))
+        zero(nc.gpsimd, flat(w2s))
+        load_x_words(0)
         load_x_scales()
         nc.sync.dma_start(slot_list[:], offs)
-        load_x_words()
+        load_x_words(1)
         load_w1_words(0, 2)
-        load_w1_scales(0, 2)
-        gather_scales(*SCALE_MOVES[0], nc.scalar)
-        load_w1_words(2, 5)
-        load_w1_scales(2, 5)
-        gather_scales(*SCALE_MOVES[1], nc.scalar)
+        load_w1_scales(0, 4)
+        for run in SCALE_MOVES[:2]:
+            gather_scales(*run)
+            move_scales(run[0], nc.scalar)
         for run in WORD_RUNS[:3]:
             gather_words(*run)
-        load_w1_words(5, 9)
-        load_w1_scales(5, 9)
+        gather_scales(*SCALE_MOVES[2])
+        for run in WORD_RUNS[3:]:
+            gather_words(*run)
+        load_w1_words(2, 4)
+        load_w1_words(4, 6)
+        load_w1_words(6, 8)
+        load_w1_scales(4, 8)
+        load_w1_words(8, 10)
+        move_scales(7, nc.sync)
+        load_w1_words(10, 12)
+        load_w1_scales(8, 12)
+        load_w2_scales()
+        for run in W2_WORD_LOADS:
+            load_w2_words(*run)
+        for lst, src in zip(pos_lists, (pos1, pos2, pos3)):
+            nc.sync.dma_start(lst[:], src)
+        nc.sync.dma_start(out=gates[:], in_=gate.rearrange("r n t -> n r t"))
 
-        def first_layer(e0, e1):
-            for e in range(e0, e1):
-                a = banks.tile([P, H], F32, name="a", tag=("even%d", "odd%d")[e % 2] % (e // 2 % 3))
-                for o in range(PASSES):
-                    nc.tensor.matmul_mx(
-                        out=a[:],
-                        lhsT=token_words[e][o].bitcast(FP8X4),
-                        lhsT_scale=token_scales[e][o],
-                        rhs=record(w1w, W1_WORD_LOADS, e, o).bitcast(FP4X4),
-                        rhs_scale=record(w1s, W1_SCALE_LOADS, e, o),
-                        start=(o == 0),
-                        stop=(o == PASSES - 1),
-                    )
-                nc.scalar.activation(
-                    h_rows[e][:].rearrange("c (u p d) -> c u p d", u=2, d=2),
-                    a[:].rearrange("c (p u d) -> c u p d", u=2, d=2),
-                    GELU,
+        def first_layer(e):
+            a = banks.tile([P, H], F32, name="a", tag=A_BANKS[e])
+            for o in range(PASSES):
+                nc.tensor.matmul_mx(
+                    out=a[:],
+                    lhsT=token_words[e][o].bitcast(FP8X4),
+                    lhsT_scale=token_scales(e, o),
+                    rhs=record(w1w, W1_WORD_LOADS, e, o).bitcast(FP4X4),
+                    rhs_scale=record(w1s, W1_SCALE_LOADS, e, o),
+                    start=(o == 0),
+                    stop=(o == PASSES - 1),
                 )
+            nc.scalar.activation(
+                h_rows[e][:].rearrange("c (u p d) -> c u p d", u=2, d=2),
+                a[:].rearrange("c (p u d) -> c u p d", u=2, d=2),
+                GELU,
+            )
 
         def turn(g):
             e0, e1 = H_GROUPS[g]
@@ -193,7 +215,7 @@ def tile_moe_pkd_mlp_gelu_kernel(
                 words = h_rows[e][:].bitcast(F32)
                 for u in range(2):
                     nc.tensor.transpose(turned[:, e - e0, u, :], words[:, u * P : (u + 1) * P], ident[:])
-            q0 = max(a for a, b in Q_GROUPS if a <= e0)
+            q0 = first_of(Q_GROUPS, e0)
             dst = h_in[q0][:, (e0 - q0) * H : (e1 - q0) * H].bitcast(F32)
             copy = nc.vector.tensor_copy if e0 in TURN_ON_VECTOR else nc.scalar.copy
             copy(
@@ -212,9 +234,10 @@ def tile_moe_pkd_mlp_gelu_kernel(
             y = banks.tile([P, (e1 - e0) * C], F32, name="y", tag=Y_BANKS[g])
             for e in range(e0, e1):
                 own = slice(e * C, (e + 1) * C)
+                w0 = first_of(W2_WORD_LOADS, e)
                 nc.tensor.matmul_mx(
                     out=y[:, (e - e0) * C : (e - e0 + 1) * C],
-                    lhsT=w2w[:, e, :].bitcast(FP4X4),
+                    lhsT=w2w[w0][:, e - w0, :].bitcast(FP4X4),
                     lhsT_scale=w2s[:, e, :],
                     rhs=h_codes[:, own].bitcast(FP8X4),
                     rhs_scale=h_scales[:, own],
@@ -226,22 +249,11 @@ def tile_moe_pkd_mlp_gelu_kernel(
             else:
                 nc.scalar.copy(y_slots[:, cols], y[:])
 
-        first_layer(*H_GROUPS[0])
-        gather_scales(*SCALE_MOVES[2], nc.sync)
-        for run in WORD_RUNS[3:]:
-            gather_words(*run)
-        load_w1_words(9, 12)
-        load_w1_scales(9, 12)
-        load_w2_words()
-        load_w2_scales()
-        for lst, src in zip(pos_lists, (pos1, pos2, pos3)):
-            nc.sync.dma_start(lst[:], src)
-        for g in range(1, len(H_GROUPS)):
-            first_layer(*H_GROUPS[g])
-            turn(g - 1)
-        turn(len(H_GROUPS) - 1)
-        gates = keep.tile([P, 3, T], F32, name="gates", align_bytes=64)
-        nc.sync.dma_start(out=gates[:], in_=gate.rearrange("r n t -> n r t"))
+        for experts, groups in (((0, 4), (0, 1)), ((4, 8), (1, 3)), ((8, 12), (3, 7))):
+            for e in range(*experts):
+                first_layer(e)
+            for g in range(*groups):
+                turn(g)
         for g in range(len(Q_GROUPS)):
             second_layer(g)
 
@@ -255,7 +267,7 @@ def tile_moe_pkd_mlp_gelu_kernel(
                     parts[k][r][:], y_slots[:].indirect(picks), gates[:, r, k * half : (k + 1) * half], MULT
                 )
 
-        summed = banks.tile([P, blocks, P], F32, name="summed", tag="spare0")
+        summed = banks.tile([P, blocks, P], F32, name="summed", tag="b1")
         for b in range(blocks):
             for r in range(3):
                 nc.tensor.matmul(
@@ -264,7 +276,7 @@ def tile_moe_pkd_mlp_gelu_kernel(
                 )
         by_token = keep.tile([P, blocks, P], F32, name="by_token")
         nc.scalar.copy(by_token[:], summed[:])
-        back = banks.tile([P, blocks, P], F32, name="back", tag="spare1")
+        back = banks.tile([P, blocks, P], F32, name="back", tag="b2")
         for b in range(blocks):
             nc.tensor.transpose(back[:, b, :], by_token[:, b, :], ident[:])
         first = keep.tile([P, half], F32, name="first")

@@ -64,7 +64,7 @@ def tile_moe_pkd_mlp_gelu_kernel(
         w2w = {
             e0: keep.tile([P, e1 - e0, 2 * N], U8, name="w2w%d" % e0, align_bytes=64) for e0, e1 in W2_WORD_LOADS
         }
-        w2s = keep.tile([P, E, N], U8, name="w2s", align_bytes=64)
+        w2s = w1s[0][:].rearrange("p a b -> p (a b)")[:, : E * N].rearrange("p (e n) -> p e n", n=N)
         ident = keep.tile([P, P], F32, name="ident", align_bytes=64)
         h_in = {
             e0: keep.tile([P, (e1 - e0) * H], BF16, name="h_in%d" % e0, align_bytes=64) for e0, e1 in Q_GROUPS
@@ -157,10 +157,9 @@ def tile_moe_pkd_mlp_gelu_kernel(
         zero(nc.vector, moved[0][:])
         zero(nc.vector, moved[2][:])
         zero(nc.vector, flat(w1s[4]))
-        zero(nc.gpsimd, flat(w1s[8]))
-        zero(nc.gpsimd, moved[7][:])
+        zero(nc.vector, flat(w1s[8]))
+        zero(nc.vector, moved[7][:])
         make_identity(nc, ident[:])
-        zero(nc.gpsimd, flat(w2s))
         load_x_words(0)
         load_x_scales()
         nc.sync.dma_start(slot_list[:], offs)
@@ -183,12 +182,6 @@ def tile_moe_pkd_mlp_gelu_kernel(
         move_scales(7, nc.sync)
         load_w1_words(10, 12)
         load_w1_scales(8, 12)
-        load_w2_scales()
-        for run in W2_WORD_LOADS:
-            load_w2_words(*run)
-        for lst, src in zip(pos_lists, (pos1, pos2, pos3)):
-            nc.sync.dma_start(lst[:], src)
-        nc.sync.dma_start(out=gates[:], in_=gate.rearrange("r n t -> n r t"))
 
         def first_layer(e):
             a = banks.tile([P, H], F32, name="a", tag=A_BANKS[e])
@@ -249,11 +242,21 @@ def tile_moe_pkd_mlp_gelu_kernel(
             else:
                 nc.scalar.copy(y_slots[:, cols], y[:])
 
-        for experts, groups in (((0, 4), (0, 1)), ((4, 8), (1, 3)), ((8, 12), (3, 7))):
+        def chunk(experts, groups):
             for e in range(*experts):
                 first_layer(e)
             for g in range(*groups):
                 turn(g)
+
+        chunk((0, 4), (0, 1))
+        load_w2_scales()
+        for run in W2_WORD_LOADS:
+            load_w2_words(*run)
+        for lst, src in zip(pos_lists, (pos1, pos2, pos3)):
+            nc.sync.dma_start(lst[:], src)
+        nc.sync.dma_start(out=gates[:], in_=gate.rearrange("r n t -> n r t"))
+        chunk((4, 8), (1, 3))
+        chunk((8, 12), (3, 7))
         for g in range(len(Q_GROUPS)):
             second_layer(g)
 

@@ -58,13 +58,14 @@ def tile_moe_pkd_mlp_gelu_kernel(
         }
         w1s = {
             e0: keep.tile([P, (e1 - e0) * PASSES, H], U8, name="w1s%d" % e0, align_bytes=64)
-            for e0, e1 in W1_SCALE_LOADS
+            for e0, e1 in W1_SCALE_LOADS[:2]
         }
+        w1s[8] = w1s[0]
         h_rows = [keep.tile([P, H], BF16, name="h_rows%d" % e, align_bytes=64) for e in range(E)]
         w2w = {
             e0: keep.tile([P, e1 - e0, 2 * N], U8, name="w2w%d" % e0, align_bytes=64) for e0, e1 in W2_WORD_LOADS
         }
-        w2s = w1s[0][:].rearrange("p a b -> p (a b)")[:, : E * N].rearrange("p (e n) -> p e n", n=N)
+        w2s = keep.tile([P, E, N], U8, name="w2s", align_bytes=64)
         ident = keep.tile([P, P], F32, name="ident", align_bytes=64)
         h_in = {
             e0: keep.tile([P, (e1 - e0) * H], BF16, name="h_in%d" % e0, align_bytes=64) for e0, e1 in Q_GROUPS
@@ -157,8 +158,8 @@ def tile_moe_pkd_mlp_gelu_kernel(
         zero(nc.vector, moved[0][:])
         zero(nc.vector, moved[2][:])
         zero(nc.vector, flat(w1s[4]))
-        zero(nc.vector, flat(w1s[8]))
         zero(nc.vector, moved[7][:])
+        zero(nc.vector, flat(w2s))
         make_identity(nc, ident[:])
         load_x_words(0)
         load_x_scales()
@@ -181,7 +182,6 @@ def tile_moe_pkd_mlp_gelu_kernel(
         load_w1_words(8, 10)
         move_scales(7, nc.sync)
         load_w1_words(10, 12)
-        load_w1_scales(8, 12)
 
         def first_layer(e):
             a = banks.tile([P, H], F32, name="a", tag=A_BANKS[e])
@@ -249,6 +249,7 @@ def tile_moe_pkd_mlp_gelu_kernel(
                 turn(g)
 
         chunk((0, 4), (0, 1))
+        load_w1_scales(8, 12)
         load_w2_scales()
         for run in W2_WORD_LOADS:
             load_w2_words(*run)
@@ -288,6 +289,9 @@ def tile_moe_pkd_mlp_gelu_kernel(
 
         pair = keep.tile([P, half], F32, name="pair")
         second = keep.tile([P, half], F32, name="second")
-        nc.vector.tensor_tensor(pair[:], parts[1][0][:], parts[1][1][:], ADD)
-        nc.vector.tensor_tensor(second[:], pair[:], parts[1][2][:], ADD)
+        quarters = [slice(0, half // 2), slice(half // 2, half)]
+        for cols in quarters:
+            nc.vector.tensor_tensor(pair[:, cols], parts[1][0][:, cols], parts[1][1][:, cols], ADD)
+        for cols in quarters:
+            nc.vector.tensor_tensor(second[:, cols], pair[:, cols], parts[1][2][:, cols], ADD)
         nc.sync.dma_start(out=out[:, half:], in_=second[:])

@@ -12,6 +12,7 @@ U8 = mybir.dt.uint8
 FP8X4 = mybir.dt.float8_e4m3fn_x4
 FP4X4 = mybir.dt.float4_e2m1fn_x4
 GELU = mybir.ActivationFunctionType.Gelu_apprx_tanh
+COPY = mybir.ActivationFunctionType.Copy
 MULT = mybir.AluOpType.mult
 ADD = mybir.AluOpType.add
 
@@ -264,22 +265,28 @@ def tile_moe_pkd_mlp_gelu_kernel(
         half = T // 2
         blocks = half // P
         parts = [[keep.tile([P, half], F32, name="part%d_%d" % (k, r)) for r in range(3)] for k in range(2)]
+
+        def picks(k, r):
+            return y_slots[:].indirect(pos_lists[r][:, k * half // 16 : (k + 1) * half // 16])
+
+        fetched = {}
+        for k, r in [(0, 2), (1, 1), (1, 2)]:
+            fetched[k, r] = keep.tile([P, half], F32, name="fetched%d_%d" % (k, r))
+            nc.scalar.activation(fetched[k, r][:], picks(k, r), COPY)
         for k in range(2):
             for r in range(3):
-                picks = pos_lists[r][:, k * half // 16 : (k + 1) * half // 16]
-                nc.vector.tensor_tensor(
-                    parts[k][r][:], y_slots[:].indirect(picks), gates[:, r, k * half : (k + 1) * half], MULT
-                )
+                source = fetched[k, r][:] if (k, r) in fetched else picks(k, r)
+                nc.vector.tensor_tensor(parts[k][r][:], source, gates[:, r, k * half : (k + 1) * half], MULT)
 
-        summed = banks.tile([P, blocks, P], F32, name="summed", tag="b1")
+        by_token = keep.tile([P, blocks, P], F32, name="by_token")
         for b in range(blocks):
+            summed = banks.tile([P, P], F32, name="summed", tag="b%d" % (1 + 2 * b))
             for r in range(3):
                 nc.tensor.matmul(
-                    summed[:, b, :], parts[0][r][:, b * P : (b + 1) * P], ident[:],
+                    summed[:], parts[0][r][:, b * P : (b + 1) * P], ident[:],
                     start=(r == 0), stop=(r == 2), is_transpose=True,
                 )
-        by_token = keep.tile([P, blocks, P], F32, name="by_token")
-        nc.scalar.copy(by_token[:], summed[:])
+            nc.scalar.copy(by_token[:, b, :], summed[:])
         back = banks.tile([P, blocks, P], F32, name="back", tag="b2")
         for b in range(blocks):
             nc.tensor.transpose(back[:, b, :], by_token[:, b, :], ident[:])

@@ -28,16 +28,16 @@ WINDOW = 1024
 FLOPS = 2 * SLOTS * (1024 * H + H * N)
 
 SCALE_MOVES = [(0, 2), (2, 7), (7, 12)]
-WORD_RUNS = [(0, 1), (1, 2), (2, 4), (4, 6), (6, 8), (8, 10), (10, 12)]
-W1_WORD_LOADS = [(0, 2), (2, 4), (4, 6), (6, 8), (8, 10), (10, 12)]
+WORD_RUNS = [(0, 1), (1, 2), (2, 4), (4, 6), (6, 8), (8, 10), (10, 11), (11, 12)]
+W1_WORD_LOADS = [(0, 4), (4, 6), (6, 8), (8, 10), (10, 12)]
 W1_SCALE_LOADS = [(0, 4), (4, 8), (8, 12)]
-W2_WORD_LOADS = [(0, 6), (6, 12)]
+W2_WORD_LOADS = [(0, 12)]
 H_GROUPS = [(0, 2), (2, 4), (4, 6), (6, 8), (8, 10), (10, 11), (11, 12)]
 A_BANKS = ["b0", "b1", "b2", "b3", "b4", "b5", "b6", "b7", "b0", "b1", "b3", "b6"]
 TURN_BANKS = ["b2", "b4", "b5", "b0", "b7", "b1", "b2"]
 Q_GROUPS = [(0, 4), (4, 6), (6, 8), (8, 10), (10, 11), (11, 12)]
 Y_BANKS = ["b4", "b5", "b3", "b6", "b0", "b7"]
-Y_ON_VECTOR = (11,)
+Y_ON_VECTOR = (0, 11)
 TURN_ON_VECTOR = (4, 6, 10)
 
 
@@ -74,7 +74,7 @@ def tile_moe_pkd_mlp_gelu_kernel(
         h_codes = keep.tile([P, SLOTS], U32, name="h_codes", align_bytes=64)
         h_scales = keep.tile([P, SLOTS], U8, name="h_scales", align_bytes=64)
         y_slots = keep.tile([P, SLOTS], F32, name="y_slots")
-        gates = keep.tile([P, 3, T], F32, name="gates", align_bytes=64)
+        gates = [keep.tile([P, 3, T // 2], F32, name="gates%d" % k, align_bytes=64) for k in range(2)]
         both = {
             e0: keep.tile([P, (e1 - e0) * C], U8, name="both%d" % e0, align_bytes=64) for e0, e1 in SCALE_MOVES
         }
@@ -166,7 +166,7 @@ def tile_moe_pkd_mlp_gelu_kernel(
         load_x_scales()
         nc.sync.dma_start(slot_list[:], offs)
         load_x_words(1)
-        load_w1_words(0, 2)
+        load_w1_words(0, 4)
         load_w1_scales(0, 4)
         for run in SCALE_MOVES[:2]:
             gather_scales(*run)
@@ -176,13 +176,13 @@ def tile_moe_pkd_mlp_gelu_kernel(
         gather_scales(*SCALE_MOVES[2])
         for run in WORD_RUNS[3:]:
             gather_words(*run)
-        load_w1_words(2, 4)
         load_w1_words(4, 6)
         load_w1_words(6, 8)
         load_w1_scales(4, 8)
         load_w1_words(8, 10)
         move_scales(7, nc.sync)
         load_w1_words(10, 12)
+        nc.sync.dma_start(pos_lists[0][:], pos1)
 
         def first_layer(e):
             a = banks.tile([P, H], F32, name="a", tag=A_BANKS[e])
@@ -251,12 +251,14 @@ def tile_moe_pkd_mlp_gelu_kernel(
 
         chunk((0, 4), (0, 1))
         load_w1_scales(8, 12)
-        load_w2_scales()
         for run in W2_WORD_LOADS:
             load_w2_words(*run)
-        for lst, src in zip(pos_lists, (pos1, pos2, pos3)):
+        load_w2_scales()
+        for lst, src in zip(pos_lists[1:], (pos2, pos3)):
             nc.sync.dma_start(lst[:], src)
-        nc.sync.dma_start(out=gates[:], in_=gate.rearrange("r n t -> n r t"))
+        for k in range(2):
+            columns = gate[:, :, k * T // 2 : (k + 1) * T // 2]
+            nc.sync.dma_start(out=gates[k][:], in_=columns.rearrange("r n t -> n r t"))
         chunk((4, 8), (1, 3))
         chunk((8, 12), (3, 7))
         for g in range(len(Q_GROUPS)):
@@ -276,7 +278,7 @@ def tile_moe_pkd_mlp_gelu_kernel(
         for k in range(2):
             for r in range(3):
                 source = fetched[k, r][:] if (k, r) in fetched else picks(k, r)
-                nc.vector.tensor_tensor(parts[k][r][:], source, gates[:, r, k * half : (k + 1) * half], MULT)
+                nc.vector.tensor_tensor(parts[k][r][:], source, gates[k][:, r, :], MULT)
 
         by_token = keep.tile([P, blocks, P], F32, name="by_token")
         for b in range(blocks):

from contextlib import ExitStack

import concourse.mybir as mybir
from concourse.masks import make_identity

F32 = mybir.dt.float32
BF16 = mybir.dt.bfloat16
I32 = mybir.dt.int32
U32 = mybir.dt.uint32
U16 = mybir.dt.uint16
U8 = mybir.dt.uint8
FP8X4 = mybir.dt.float8_e4m3fn_x4
FP4X4 = mybir.dt.float4_e2m1fn_x4
GELU = mybir.ActivationFunctionType.Gelu_apprx_tanh
COPY = mybir.ActivationFunctionType.Copy
MULT = mybir.AluOpType.mult
ADD = mybir.AluOpType.add

P = 128
T, E, C, H, N = 512, 12, 128, 512, 128
PASSES = 2
SLOTS = E * C
LIST_COLS = C // 16
LIVE = 112
SHIFT = 16
WINDOW = 1024

FLOPS = 2 * SLOTS * (1024 * H + H * N)

SCALE_MOVES = [(0, 2), (2, 7), (7, 12)]
WORD_RUNS = [(0, 1), (1, 2), (2, 4), (4, 6), (6, 8), (8, 10), (10, 11), (11, 12)]
W1_WORD_LOADS = [(0, 4), (4, 6), (6, 8), (8, 10), (10, 12)]
W1_SCALE_LOADS = [(0, 4), (4, 8), (8, 12)]
W2_WORD_LOADS = [(0, 12)]
H_GROUPS = [(0, 2), (2, 4), (4, 6), (6, 8), (8, 10), (10, 11), (11, 12)]
A_BANKS = ["b0", "b1", "b2", "b3", "b4", "b5", "b6", "b7", "b0", "b1", "b3", "b6"]
TURN_BANKS = ["b2", "b4", "b5", "b0", "b7", "b1", "b2"]
Q_GROUPS = [(0, 4), (4, 6), (6, 8), (8, 10), (10, 11), (11, 12)]
Y_BANKS = ["b4", "b5", "b3", "b6", "b0", "b7"]
Y_ON_VECTOR = (0, 11)
TURN_ON_VECTOR = (4, 6, 10)


def tile_moe_pkd_mlp_gelu_kernel(
    tc, x_words, x_scales, w1_words, w1_scales, w2_words, w2_scales, gate, offs, pos1, pos2, pos3, out
):
    nc = tc.nc
    with ExitStack() as ctx:
        keep = ctx.enter_context(tc.tile_pool(name="keep", bufs=1))
        banks = ctx.enter_context(tc.psum_pool(name="banks", bufs=1))

        slot_list = keep.tile([P, E * LIST_COLS], U16, name="slot_list")
        pos_lists = [keep.tile([P, T // 16], U16, name="pos%d" % r) for r in range(3)]
        xw = [keep.tile([P, T], I32, name="xw%d" % o, align_bytes=64) for o in range(PASSES)]
        xs = keep.tile([P, WINDOW], U8, name="xs", align_bytes=64)
        w1w = {
            e0: keep.tile([P, (e1 - e0) * PASSES, 2 * H], U8, name="w1w%d" % e0, align_bytes=64)
            for e0, e1 in W1_WORD_LOADS
        }
        w1s = {
            e0: keep.tile([P, (e1 - e0) * PASSES, H], U8, name="w1s%d" % e0, align_bytes=64)
            for e0, e1 in W1_SCALE_LOADS[:2]
        }
        w1s[8] = w1s[0]
        h_rows = [keep.tile([P, H], BF16, name="h_rows%d" % e, align_bytes=64) for e in range(E)]
        w2w = {
            e0: keep.tile([P, e1 - e0, 2 * N], U8, name="w2w%d" % e0, align_bytes=64) for e0, e1 in W2_WORD_LOADS
        }
        w2s = keep.tile([P, E, N], U8, name="w2s", align_bytes=64)
        ident = keep.tile([P, P], F32, name="ident", align_bytes=64)
        h_in = {
            e0: keep.tile([P, (e1 - e0) * H], BF16, name="h_in%d" % e0, align_bytes=64) for e0, e1 in Q_GROUPS
        }
        h_codes = keep.tile([P, SLOTS], U32, name="h_codes", align_bytes=64)
        h_scales = keep.tile([P, SLOTS], U8, name="h_scales", align_bytes=64)
        y_slots = keep.tile([P, SLOTS], F32, name="y_slots")
        gates = [keep.tile([P, 3, T // 2], F32, name="gates%d" % k, align_bytes=64) for k in range(2)]
        both = {
            e0: keep.tile([P, (e1 - e0) * C], U8, name="both%d" % e0, align_bytes=64) for e0, e1 in SCALE_MOVES
        }
        moved = {
            e0: keep.tile([P, (e1 - e0) * C], U8, name="moved%d" % e0, align_bytes=64) for e0, e1 in SCALE_MOVES
        }

        def first_of(groups, e):
            return max(a for a, b in groups if a <= e)

        def record(tiles, loads, e, o):
            e0 = first_of(loads, e)
            return tiles[e0][:, (e - e0) * PASSES + o, :]

        def load_w1_scales(e0, e1):
            for r in range(4):
                nc.sync.dma_start(
                    out=w1s[e0][r:P:32].bitcast(I32),
                    in_=w1_scales[e0:e1, :, r:16:4, :].rearrange("e s q i -> q (e s) i").bitcast(I32),
                )

        def load_w1_words(e0, e1):
            nc.sync.dma_start(
                out=w1w[e0][:].bitcast(I32),
                in_=w1_words[e0:e1].rearrange("e s p b -> p (e s) b").bitcast(I32),
            )

        def zero(engine, tile):
            engine.memset(tile.bitcast(I32), 0)

        def flat(tile):
            return tile[:].rearrange("p a b -> p (a b)")

        def load_x_scales():
            for r in range(4):
                nc.sync.dma_start(
                    out=xs[r:P:SHIFT, :T].bitcast(I32),
                    in_=x_scales[:, r:16:4, :].rearrange("o q t -> q o t").bitcast(I32),
                )

        def load_x_words(o):
            nc.sync.dma_start(out=xw[o][:], in_=x_words[o].rearrange("p t r -> p (t r)").bitcast(I32))

        def load_w2_scales():
            for r in range(4):
                nc.sync.dma_start(
                    out=w2s[r:P:32].bitcast(I32),
                    in_=w2_scales[:, 0, r:16:4, :].rearrange("e q n -> q e n").bitcast(I32),
                )

        def load_w2_words(e0, e1):
            nc.sync.dma_start(
                out=w2w[e0][:].bitcast(I32), in_=w2_words[e0:e1, 0].rearrange("e p b -> p e b").bitcast(I32)
            )

        token_words = {}

        def entries(e0, e1):
            return slot_list[:, e0 * LIST_COLS : e1 * LIST_COLS]

        def gather_scales(e0, e1):
            nc.vector.tensor_copy(both[e0][:], xs[:].indirect(entries(e0, e1)))

        def move_scales(e0, queue):
            queue.dma_start(out=moved[e0][:LIVE].bitcast(I32), in_=both[e0][SHIFT : LIVE + SHIFT].bitcast(I32))

        def token_scales(e, o):
            e0 = first_of(SCALE_MOVES, e)
            return (both, moved)[o][e0][:, (e - e0) * C : (e - e0 + 1) * C]

        def gather_words(e0, e1):
            gw = keep.tile([P, PASSES, (e1 - e0) * C], I32, name="gw%d" % e0, align_bytes=64)
            for o in range(PASSES):
                nc.vector.tensor_copy(gw[:, o, :].bitcast(U32), xw[o][:].bitcast(U32).indirect(entries(e0, e1)))
            for e in range(e0, e1):
                cols = slice((e - e0) * C, (e - e0 + 1) * C)
                token_words[e] = [gw[:, o, cols] for o in range(PASSES)]

        zero(nc.gpsimd, xs[:])
        zero(nc.gpsimd, flat(w1s[0])[:, : 4 * H])
        zero(nc.vector, flat(w1s[0])[:, 4 * H :])
        zero(nc.vector, moved[0][:])
        zero(nc.vector, moved[2][:])
        zero(nc.vector, flat(w1s[4]))
        zero(nc.vector, moved[7][:])
        zero(nc.vector, flat(w2s))
        make_identity(nc, ident[:])
        load_x_words(0)
        load_x_scales()
        nc.sync.dma_start(slot_list[:], offs)
        load_x_words(1)
        load_w1_words(0, 4)
        load_w1_scales(0, 4)
        for run in SCALE_MOVES[:2]:
            gather_scales(*run)
            move_scales(run[0], nc.scalar)
        for run in WORD_RUNS[:3]:
            gather_words(*run)
        gather_scales(*SCALE_MOVES[2])
        for run in WORD_RUNS[3:]:
            gather_words(*run)
        load_w1_words(4, 6)
        load_w1_words(6, 8)
        load_w1_scales(4, 8)
        load_w1_words(8, 10)
        move_scales(7, nc.sync)
        load_w1_words(10, 12)
        nc.sync.dma_start(pos_lists[0][:], pos1)

        def first_layer(e):
            a = banks.tile([P, H], F32, name="a", tag=A_BANKS[e])
            for o in range(PASSES):
                nc.tensor.matmul_mx(
                    out=a[:],
                    lhsT=token_words[e][o].bitcast(FP8X4),
                    lhsT_scale=token_scales(e, o),
                    rhs=record(w1w, W1_WORD_LOADS, e, o).bitcast(FP4X4),
                    rhs_scale=record(w1s, W1_SCALE_LOADS, e, o),
                    start=(o == 0),
                    stop=(o == PASSES - 1),
                )
            nc.scalar.activation(
                h_rows[e][:].rearrange("c (u p d) -> c u p d", u=2, d=2),
                a[:].rearrange("c (p u d) -> c u p d", u=2, d=2),
                GELU,
            )

        def turn(g):
            e0, e1 = H_GROUPS[g]
            turned = banks.tile([P, e1 - e0, 2, C], F32, name="turned", tag=TURN_BANKS[g])
            for e in range(e0, e1):
                words = h_rows[e][:].bitcast(F32)
                for u in range(2):
                    nc.tensor.transpose(turned[:, e - e0, u, :], words[:, u * P : (u + 1) * P], ident[:])
            q0 = first_of(Q_GROUPS, e0)
            dst = h_in[q0][:, (e0 - q0) * H : (e1 - q0) * H].bitcast(F32)
            copy = nc.vector.tensor_copy if e0 in TURN_ON_VECTOR else nc.scalar.copy
            copy(
                dst.rearrange("p (e c u) -> p e c u", u=2, c=C),
                turned[:].rearrange("p e u c -> p e c u"),
            )

        def second_layer(g):
            e0, e1 = Q_GROUPS[g]
            cols = slice(e0 * C, e1 * C)
            nc.vector.quantize_mx(
                out=h_codes[:, cols].bitcast(FP8X4),
                scales=h_scales[:, cols],
                in_=h_in[e0][:],
            )
            y = banks.tile([P, (e1 - e0) * C], F32, name="y", tag=Y_BANKS[g])
            for e in range(e0, e1):
                own = slice(e * C, (e + 1) * C)
                w0 = first_of(W2_WORD_LOADS, e)
                nc.tensor.matmul_mx(
                    out=y[:, (e - e0) * C : (e - e0 + 1) * C],
                    lhsT=w2w[w0][:, e - w0, :].bitcast(FP4X4),
                    lhsT_scale=w2s[:, e, :],
                    rhs=h_codes[:, own].bitcast(FP8X4),
                    rhs_scale=h_scales[:, own],
                    start=True,
                    stop=True,
                )
            if e0 in Y_ON_VECTOR:
                nc.vector.tensor_copy(y_slots[:, cols], y[:])
            else:
                nc.scalar.copy(y_slots[:, cols], y[:])

        def chunk(experts, groups):
            for e in range(*experts):
                first_layer(e)
            for g in range(*groups):
                turn(g)

        chunk((0, 4), (0, 1))
        load_w1_scales(8, 12)
        for run in W2_WORD_LOADS:
            load_w2_words(*run)
        load_w2_scales()
        for lst, src in zip(pos_lists[1:], (pos2, pos3)):
            nc.sync.dma_start(lst[:], src)
        for k in range(2):
            columns = gate[:, :, k * T // 2 : (k + 1) * T // 2]
            nc.sync.dma_start(out=gates[k][:], in_=columns.rearrange("r n t -> n r t"))
        chunk((4, 8), (1, 3))
        chunk((8, 12), (3, 7))
        for g in range(len(Q_GROUPS)):
            second_layer(g)

        half = T // 2
        blocks = half // P
        parts = [[keep.tile([P, half], F32, name="part%d_%d" % (k, r)) for r in range(3)] for k in range(2)]

        def picks(k, r):
            return y_slots[:].indirect(pos_lists[r][:, k * half // 16 : (k + 1) * half // 16])

        fetched = {}
        for k, r in [(0, 2), (1, 1), (1, 2)]:
            fetched[k, r] = keep.tile([P, half], F32, name="fetched%d_%d" % (k, r))
            nc.scalar.activation(fetched[k, r][:], picks(k, r), COPY)
        for k in range(2):
            for r in range(3):
                source = fetched[k, r][:] if (k, r) in fetched else picks(k, r)
                nc.vector.tensor_tensor(parts[k][r][:], source, gates[k][:, r, :], MULT)

        by_token = keep.tile([P, blocks, P], F32, name="by_token")
        for b in range(blocks):
            summed = banks.tile([P, P], F32, name="summed", tag="b%d" % (1 + 2 * b))
            for r in range(3):
                nc.tensor.matmul(
                    summed[:], parts[0][r][:, b * P : (b + 1) * P], ident[:],
                    start=(r == 0), stop=(r == 2), is_transpose=True,
                )
            nc.scalar.copy(by_token[:, b, :], summed[:])
        back = banks.tile([P, blocks, P], F32, name="back", tag="b2")
        for b in range(blocks):
            nc.tensor.transpose(back[:, b, :], by_token[:, b, :], ident[:])
        first = keep.tile([P, half], F32, name="first")
        nc.scalar.copy(first[:], back[:].rearrange("p b t -> p (b t)"))
        nc.scalar.dma_start(out=out[:, :half], in_=first[:])

        pair = keep.tile([P, half], F32, name="pair")
        second = keep.tile([P, half], F32, name="second")
        quarters = [slice(0, half // 2), slice(half // 2, half)]
        for cols in quarters:
            nc.vector.tensor_tensor(pair[:, cols], parts[1][0][:, cols], parts[1][1][:, cols], ADD)
        for cols in quarters:
            nc.vector.tensor_tensor(second[:, cols], pair[:, cols], parts[1][2][:, cols], ADD)
        nc.sync.dma_start(out=out[:, half:], in_=second[:])
